import numpy as np
import ml_dtypes


def mxq(x, axis, fmt="e4m3"):
    dtype, down = {"e4m3": (ml_dtypes.float8_e4m3fn, 7), "e5m2": (ml_dtypes.float8_e5m2, 14)}[fmt]
    v = np.moveaxis(np.asarray(x, np.float32).astype(ml_dtypes.bfloat16).astype(np.float64), axis, -1)
    blocks = v.reshape(v.shape[:-1] + (-1, 32))
    amax = np.abs(blocks).max(-1, keepdims=True)
    byte = np.maximum(np.where(amax > 0, np.frexp(amax)[1] - 1 + 127, 0) - down, 1)
    scale = np.exp2(byte - 127.0)
    codes = (blocks / scale).astype(np.float32).astype(dtype).astype(np.float64)
    return np.moveaxis((codes * scale).reshape(v.shape), -1, axis)


WIDE = False


def mx_kscale(k):
    if not WIDE:
        return np.ones(k)
    levels = np.array([10, -10, 5, -5, 0])
    if k % 512:
        return np.exp2(np.random.permutation(np.resize(levels, k // 32))).repeat(32)
    a = np.empty((k // 512, 16))
    for p in range(k // 512):
        a[p, :8] = np.random.permutation(np.resize(levels, 8))
        for g in range(8):
            far = levels[np.abs(levels - a[p, g]) >= 10]
            a[p, g + 8] = far[np.random.randint(len(far))]
    return np.exp2(a.ravel()).repeat(32)


def f64(x):
    return np.asarray(x).astype(np.float64)


def striped(idx):
    return np.tile(idx.reshape(-1, 16).T, (8, 1)).astype(np.uint16)


def unstriped(offs):
    return offs[:16].T.reshape(-1).astype(np.int64)


def pack_weight(w):
    k, n = w.shape
    w = f64(np.asarray(w, np.float32).astype(ml_dtypes.bfloat16)).reshape(k // 32, 32, n)
    amax = np.abs(w).max(1)
    byte = np.clip(np.where(amax > 0, np.frexp(amax)[1] - 1 + 127 - 7, 1), 1, 254)
    scaled = (w * np.exp2(127.0 - byte)[:, None, :]).reshape(k, n).astype(np.float32)
    words = np.ascontiguousarray(scaled.reshape(k // 512, 128, 4, n).transpose(0, 1, 3, 2)).astype(ml_dtypes.float8_e4m3fn).view(np.uint8)
    return words, np.ascontiguousarray(byte.astype(np.uint8).reshape(k // 512, 16, n))


def unpack_weight(words, scales):
    g, p, n, _ = words.shape
    vals = np.ascontiguousarray(words).view(ml_dtypes.float8_e4m3fn).astype(np.float64) * np.repeat(np.exp2(scales.astype(np.float64) - 127.0), 8, axis=1)[..., None]
    return vals.transpose(0, 1, 3, 2).reshape(g * 512, n)


def relu(v):
    return np.maximum(v, 0.0)


K, T, S, V, H, N = 512, 1024, 512, 256, 512, 128


def setup_inputs():
    n = np.random.standard_normal
    s = mx_kscale(K)[:, None]
    u = mx_kscale(H)
    packed_xT = pack_weight(n((K, T)) * s)
    packed_w2 = pack_weight(n((H, N)) / np.sqrt(2 * H) / u[:, None])
    packed_w3 = pack_weight(n((H, N)) / np.sqrt(2 * H) / u[:, None])
    return {
        "x_words": packed_xT[0],
        "x_scales": packed_xT[1],
        "w1": (n((K, H)) / np.sqrt(K) / s * u).astype(np.float32),
        "w2_words": packed_w2[0],
        "w2_scales": packed_w2[1],
        "w3_words": packed_w3[0],
        "w3_scales": packed_w3[1],
        "offs": striped(np.random.permutation(T)[:S]),
        "cen": striped(np.random.permutation(S)[:V]),
        "pos1": striped(np.random.permutation(S)[:V]),
        "pos2": striped(np.random.permutation(S)[:V]),
        "pos3": striped(np.random.permutation(S)[:V]),
    }


def reference(x_words, x_scales, w1, w2_words, w2_scales, w3_words, w3_scales, offs, cen, pos1, pos2, pos3):
    xq = unpack_weight(x_words, x_scales)[:, unstriped(offs)]
    h = relu(mxq(f64(w1), 0, "e4m3").T @ xq)
    g = h[:, unstriped(cen)]
    z = (h[:, unstriped(pos1)] + h[:, unstriped(pos2)] + h[:, unstriped(pos3)]) / 3
    return unpack_weight(w2_words, w2_scales).T @ mxq(g, 0, "e4m3") + unpack_weight(w3_words, w3_scales).T @ mxq(z, 0, "e4m3")

@@ -1,0 +1,239 @@
+from contextlib import ExitStack
+
+import concourse.mybir as mybir
+from concourse.masks import make_identity
+
+K, T, S, V, H, N = 512, 1024, 512, 256, 512, 128
+FLOPS = 2 * K * H * S + 2 * 2 * H * N * V
+
+F32 = mybir.dt.float32
+BF16 = mybir.dt.bfloat16
+I32 = mybir.dt.int32
+U32 = mybir.dt.uint32
+U16 = mybir.dt.uint16
+U8 = mybir.dt.uint8
+FP8X4 = mybir.dt.float8_e4m3fn_x4
+COPY = mybir.ActivationFunctionType.Copy
+RELU = mybir.ActivationFunctionType.Relu
+
+P = 128
+PACK = 4
+CHUNKS = H // P
+HALVES = V // P
+
+
+def load_scales(queue, plane, scales):
+    width = scales.shape[2]
+    rows = scales.bitcast(I32)
+    for q in range(4):
+        queue.dma_start(
+            out=plane[32 * q : 32 * q + 32, :].bitcast(I32),
+            in_=rows[:, 4 * q : 4 * q + 4, :].broadcast_to([8, 4, width // 4]),
+        )
+
+
+def tile_picked_sagecat_mean_p_kernel(
+    tc, x_words, x_scales, w1, w2_words, w2_scales, w3_words, w3_scales, offs, cen, pos1, pos2, pos3, out
+):
+    nc = tc.nc
+    with ExitStack() as ctx:
+        sb = ctx.enter_context(tc.tile_pool(name="sb", bufs=1))
+        ps = ctx.enter_context(tc.psum_pool(name="ps", bufs=1))
+
+        def bank(b, shape):
+            return ps.tile(shape, F32, name="bank%d" % b)
+
+        offs_t = sb.tile([P, S // 16], U16, name="offs_t")
+        nc.sync.dma_start(offs_t[:], offs)
+        xs = sb.tile([P, T], U8, name="xs", align_bytes=64)
+        load_scales(nc.scalar, xs, x_scales)
+        xw = sb.tile([P, T], I32, name="xw", align_bytes=64)
+        nc.sync.dma_start(out=xw[:], in_=x_words[0].rearrange("p n t -> p (n t)").bitcast(I32))
+        w1_rows = w1.rearrange("(p j) n -> p j n", j=PACK)
+        w1_raw = []
+        for c in range(CHUNKS):
+            raw = sb.tile([P, PACK, P], F32, name="w1_raw%d" % c)
+            nc.sync.dma_start(out=raw[:], in_=w1_rows[:, :, c * P : (c + 1) * P])
+            w1_raw.append(raw)
+        pos_t = []
+        for d, pos in enumerate((pos1, pos2, pos3)):
+            t = sb.tile([P, V // 16], U16, name="pos_t%d" % d)
+            nc.sync.dma_start(t[:], pos)
+            pos_t.append(t)
+        cen_t = sb.tile([P, V // 16], U16, name="cen_t")
+        nc.sync.dma_start(cen_t[:], cen)
+        last_words = []
+        last_scales = []
+        for i, (words, scales) in enumerate(((w3_words, w3_scales), (w2_words, w2_scales))):
+            wt = sb.tile([P, N], I32, name="last_words%d" % i, align_bytes=64)
+            nc.sync.dma_start(out=wt[:], in_=words[0].rearrange("p n t -> p (n t)").bitcast(I32))
+            st = sb.tile([P, N], U8, name="last_scales%d" % i, align_bytes=64)
+            load_scales(nc.sync, st, scales)
+            last_words.append(wt)
+            last_scales.append(st)
+
+        ident = sb.tile([P, P], F32, name="ident")
+        make_identity(nc, ident[:])
+
+        w1_bf = [sb.tile([P, P, PACK], BF16, name="w1_bf%d" % c, align_bytes=64) for c in range(CHUNKS)]
+        w1_codes = [sb.tile([P, P], U32, name="w1_codes%d" % c, align_bytes=64) for c in range(CHUNKS)]
+        w1_scales = [sb.tile([P, P], U8, name="w1_scales%d" % c, align_bytes=64) for c in range(CHUNKS)]
+
+        def round_w1(c):
+            nc.scalar.activation(
+                out=w1_bf[c][:].rearrange("p (n i) j -> p n j i", i=4),
+                in_=w1_raw[c][:].rearrange("p j (n i) -> p n j i", i=4),
+                func=COPY,
+            )
+
+        def quantize_w1(c):
+            nc.vector.quantize_mx(
+                out=w1_codes[c][:].bitcast(FP8X4),
+                scales=w1_scales[c][:],
+                in_=w1_bf[c][:].rearrange("p n j -> p (n j)"),
+            )
+
+        picked_scales = sb.tile([P, S], U8, name="picked_scales", align_bytes=64)
+        picked_words = sb.tile([P, S], U32, name="picked_words", align_bytes=64)
+        h = [sb.tile([P, S], F32, name="h%d" % c) for c in range(CHUNKS)]
+
+        def first_layer(c, b, cols):
+            acc = bank(b, [P, cols.stop - cols.start])
+            nc.tensor.matmul_mx(
+                out=acc[:],
+                lhsT=w1_codes[c][:].bitcast(FP8X4),
+                lhsT_scale=w1_scales[c][:],
+                rhs=picked_words[:, cols].bitcast(FP8X4),
+                rhs_scale=picked_scales[:, cols],
+                start=True,
+                stop=True,
+            )
+            nc.scalar.activation(out=h[c][:, cols], in_=acc[:], func=RELU)
+
+        nc.vector.tensor_copy(picked_scales[:], xs[:].indirect(offs_t[:]))
+        round_w1(0)
+        half = S // 2
+        nc.vector.tensor_copy(picked_words[:, :half], xw[:].bitcast(U32).indirect(offs_t[:, : half // 16]))
+        quantize_w1(0)
+        first_layer(0, 0, slice(0, half))
+        nc.vector.tensor_copy(picked_words[:, half:], xw[:].bitcast(U32).indirect(offs_t[:, half // 16 :]))
+        round_w1(1)
+        first_layer(0, 1, slice(half, S))
+        quantize_w1(1)
+        round_w1(2)
+        first_layer(1, 2, slice(0, S))
+        quantize_w1(2)
+        round_w1(3)
+        first_layer(2, 0, slice(0, S))
+        quantize_w1(3)
+        first_layer(3, 1, slice(0, S))
+
+        z_rows = [sb.tile([P, 2, P, 2], BF16, name="z_rows%d" % b) for b in range(HALVES)]
+        g_rows = [sb.tile([P, 2, P, 2], BF16, name="g_rows%d" % b) for b in range(HALVES)]
+
+        def in_word_order(turned):
+            return turned.rearrange("v (p u e) -> v u p e", u=2, e=2)
+
+        def sum_neighbours(chunks, banks):
+            turned = [bank(bk, [P, len(chunks) * P]) for bk in banks]
+            for i, c in enumerate(chunks):
+                for d in range(3):
+                    f = sb.tile([P, V], F32, name="fetched%d_%d" % (c, d))
+                    fetched[c, d] = f
+                    nc.vector.tensor_copy(f[:], h[c][:].indirect(pos_t[d][:]))
+                    for b in range(HALVES):
+                        nc.tensor.matmul(
+                            turned[b][:, i * P : (i + 1) * P],
+                            lhsT=f[:, b * P : (b + 1) * P],
+                            rhs=ident[:],
+                            is_transpose=True,
+                            start=(d == 0),
+                            stop=(d == 2),
+                        )
+                if c < 2:
+                    f = sb.tile([P, V], F32, name="centre%d" % c)
+                    nc.vector.tensor_copy(f[:], h[c][:].indirect(cen_t[:]))
+                    for b in range(HALVES):
+                        nc.tensor.transpose(g_early[:, b, c * P : (c + 1) * P], f[:, b * P : (b + 1) * P], ident[:])
+                if c == 1:
+                    for b in range(HALVES):
+                        nc.scalar.copy(out=g_rows[b][:, :, 0:64, :], in_=in_word_order(g_early[:, b, :]))
+            for b in range(HALVES):
+                nc.scalar.activation(
+                    out=z_rows[b][:, :, 32 * chunks.start : 32 * chunks.stop, :],
+                    in_=in_word_order(turned[b][:]),
+                    func=COPY,
+                    scale=1.0 / 3.0,
+                )
+
+        fetched = {}
+        g_early = bank(5, [P, HALVES, 2 * P])
+        sum_neighbours(range(0, 3), (3, 4))
+        sum_neighbours(range(3, 4), (2, 6))
+
+        def fetch_centres(b, chunks, bk):
+            g_turned = bank(bk, [P, len(chunks) * P])
+            for i, c in enumerate(chunks):
+                slot = fetched[CHUNKS - 1, b][:, (c - 2) * P : (c - 1) * P]
+                nc.vector.tensor_copy(slot, h[c][:].indirect(cen_t[:, b * 8 : (b + 1) * 8]))
+                nc.tensor.transpose(g_turned[:, i * P : (i + 1) * P], slot, ident[:])
+            nc.scalar.copy(out=g_rows[b][:, :, 32 * chunks.start : 32 * chunks.stop, :], in_=in_word_order(g_turned[:]))
+
+        def turn_back(rows, words):
+            pairs = rows[:].rearrange("v u p e -> v (u p e)").bitcast(F32)
+            for u in range(2):
+                nc.tensor.transpose(words[:, u, :], pairs[:, u * P : (u + 1) * P], ident[:])
+
+        def centre_values(b, bk):
+            g_words = bank(bk, [P, 2, P])
+            turn_back(g_rows[b], g_words)
+            gb = sb.tile([P, P * PACK], BF16, name="g_bf%d" % b, align_bytes=64)
+            nc.scalar.copy(
+                out=gb[:].bitcast(F32).rearrange("p (v u) -> p v u", u=2),
+                in_=g_words[:].rearrange("p u v -> p v u"),
+            )
+            return gb
+
+        fetch_centres(0, range(2, 4), 0)
+        z_words = bank(5, [P, HALVES, 2, P])
+        for b in range(HALVES):
+            turn_back(z_rows[b], z_words[:, b])
+        z_bf = sb.tile([P, V * PACK], BF16, name="z_bf", align_bytes=64)
+        nc.scalar.copy(
+            out=z_bf[:].bitcast(F32).rearrange("p (b v u) -> p b v u", b=HALVES, u=2),
+            in_=z_words[:].rearrange("p b u v -> p b v u"),
+        )
+        z_codes = sb.tile([P, V], U32, name="z_codes", align_bytes=64)
+        z_scales = sb.tile([P, V], U8, name="z_scales", align_bytes=64)
+        fetch_centres(1, range(2, 3), 1)
+        fetch_centres(1, range(3, 4), 7)
+        g_bf = [centre_values(0, 3), centre_values(1, 4)]
+
+        nc.vector.quantize_mx(out=z_codes[:].bitcast(FP8X4), scales=z_scales[:], in_=z_bf[:])
+        for b in range(HALVES):
+            cols = slice(b * P, (b + 1) * P)
+            g_codes = sb.tile([P, P], U32, name="g_codes%d" % b, align_bytes=64)
+            g_scales = sb.tile([P, P], U8, name="g_scales%d" % b, align_bytes=64)
+            nc.vector.quantize_mx(out=g_codes[:].bitcast(FP8X4), scales=g_scales[:], in_=g_bf[b][:])
+            acc = bank((2, 6)[b], [P, P])
+            nc.tensor.matmul_mx(
+                out=acc[:],
+                lhsT=last_words[0][:].bitcast(FP8X4),
+                lhsT_scale=last_scales[0][:],
+                rhs=z_codes[:, cols].bitcast(FP8X4),
+                rhs_scale=z_scales[:, cols],
+                start=True,
+                stop=False,
+            )
+            nc.tensor.matmul_mx(
+                out=acc[:],
+                lhsT=last_words[1][:].bitcast(FP8X4),
+                lhsT_scale=last_scales[1][:],
+                rhs=g_codes[:].bitcast(FP8X4),
+                rhs_scale=g_scales[:],
+                start=False,
+                stop=True,
+            )
+            result = sb.tile([P, P], F32, name="result%d" % b)
+            nc.vector.tensor_copy(result[:], acc[:])
+            nc.sync.dma_start(out=out[:, cols], in_=result[:])

@@ -22,10 +22,10 @@ CHUNKS = H // P
 HALVES = V // P
 
 
-def load_scales(queue, plane, scales):
+def load_scales(queues, plane, scales):
     width = scales.shape[2]
     rows = scales.bitcast(I32)
-    for q in range(4):
+    for q, queue in enumerate(queues):
         queue.dma_start(
             out=plane[32 * q : 32 * q + 32, :].bitcast(I32),
             in_=rows[:, 4 * q : 4 * q + 4, :].broadcast_to([8, 4, width // 4]),
@@ -46,15 +46,16 @@ def tile_picked_sagecat_mean_p_kernel(
         offs_t = sb.tile([P, S // 16], U16, name="offs_t")
         nc.sync.dma_start(offs_t[:], offs)
         xs = sb.tile([P, T], U8, name="xs", align_bytes=64)
-        load_scales(nc.scalar, xs, x_scales)
+        load_scales((nc.sync, nc.scalar, nc.scalar, nc.scalar), xs, x_scales)
         xw = sb.tile([P, T], I32, name="xw", align_bytes=64)
-        nc.sync.dma_start(out=xw[:], in_=x_words[0].rearrange("p n t -> p (n t)").bitcast(I32))
         w1_rows = w1.rearrange("(p j) n -> p j n", j=PACK)
         w1_raw = []
         for c in range(CHUNKS):
             raw = sb.tile([P, PACK, P], F32, name="w1_raw%d" % c)
             nc.sync.dma_start(out=raw[:], in_=w1_rows[:, :, c * P : (c + 1) * P])
             w1_raw.append(raw)
+            if c == 0:
+                nc.sync.dma_start(out=xw[:], in_=x_words[0].rearrange("p n t -> p (n t)").bitcast(I32))
         pos_t = []
         for d, pos in enumerate((pos1, pos2, pos3)):
             t = sb.tile([P, V // 16], U16, name="pos_t%d" % d)
@@ -68,18 +69,19 @@ def tile_picked_sagecat_mean_p_kernel(
             wt = sb.tile([P, N], I32, name="last_words%d" % i, align_bytes=64)
             nc.sync.dma_start(out=wt[:], in_=words[0].rearrange("p n t -> p (n t)").bitcast(I32))
             st = sb.tile([P, N], U8, name="last_scales%d" % i, align_bytes=64)
-            load_scales(nc.sync, st, scales)
+            load_scales((nc.sync,) * 4, st, scales)
             last_words.append(wt)
             last_scales.append(st)
 
         ident = sb.tile([P, P], F32, name="ident")
         make_identity(nc, ident[:])
 
-        w1_bf = [sb.tile([P, P, PACK], BF16, name="w1_bf%d" % c, align_bytes=64) for c in range(CHUNKS)]
+        w1_bf = {}
         w1_codes = [sb.tile([P, P], U32, name="w1_codes%d" % c, align_bytes=64) for c in range(CHUNKS)]
         w1_scales = [sb.tile([P, P], U8, name="w1_scales%d" % c, align_bytes=64) for c in range(CHUNKS)]
 
         def round_w1(c):
+            w1_bf[c] = sb.tile([P, P, PACK], BF16, name="w1_bf%d" % min(c, 1), align_bytes=64)
             nc.scalar.activation(
                 out=w1_bf[c][:].rearrange("p (n i) j -> p n j i", i=4),
                 in_=w1_raw[c][:].rearrange("p j (n i) -> p n j i", i=4),
@@ -97,7 +99,7 @@ def tile_picked_sagecat_mean_p_kernel(
         picked_words = sb.tile([P, S], U32, name="picked_words", align_bytes=64)
         h = [sb.tile([P, S], F32, name="h%d" % c) for c in range(CHUNKS)]
 
-        def first_layer(c, b, cols):
+        def first_layer(c, b, cols, on_vector=False):
             acc = bank(b, [P, cols.stop - cols.start])
             nc.tensor.matmul_mx(
                 out=acc[:],
@@ -108,31 +110,67 @@ def tile_picked_sagecat_mean_p_kernel(
                 start=True,
                 stop=True,
             )
-            nc.scalar.activation(out=h[c][:, cols], in_=acc[:], func=RELU)
+            if on_vector:
+                nc.vector.tensor_scalar_max(h[c][:, cols], acc[:], 0.0)
+            else:
+                nc.scalar.activation(out=h[c][:, cols], in_=acc[:], func=RELU)
 
         nc.vector.tensor_copy(picked_scales[:], xs[:].indirect(offs_t[:]))
         round_w1(0)
-        half = S // 2
-        nc.vector.tensor_copy(picked_words[:, :half], xw[:].bitcast(U32).indirect(offs_t[:, : half // 16]))
         quantize_w1(0)
-        first_layer(0, 0, slice(0, half))
-        nc.vector.tensor_copy(picked_words[:, half:], xw[:].bitcast(U32).indirect(offs_t[:, half // 16 :]))
-        round_w1(1)
-        first_layer(0, 1, slice(half, S))
-        quantize_w1(1)
-        round_w1(2)
-        first_layer(1, 2, slice(0, S))
-        quantize_w1(2)
-        round_w1(3)
-        first_layer(2, 0, slice(0, S))
-        quantize_w1(3)
-        first_layer(3, 1, slice(0, S))
+        for b, cols in enumerate((slice(0, 256), slice(256, 384), slice(384, 512))):
+            nc.vector.tensor_copy(
+                picked_words[:, cols], xw[:].bitcast(U32).indirect(offs_t[:, cols.start // 16 : cols.stop // 16])
+            )
+            first_layer(0, b, cols, on_vector=(b == 2))
+        for c, b in ((1, 6), (2, 0), (3, 1)):
+            round_w1(c)
+            quantize_w1(c)
+            first_layer(c, b, slice(0, S))
 
-        z_rows = [sb.tile([P, 2, P, 2], BF16, name="z_rows%d" % b) for b in range(HALVES)]
-        g_rows = [sb.tile([P, 2, P, 2], BF16, name="g_rows%d" % b) for b in range(HALVES)]
+        z_rows = [sb.tile([P, H], BF16, name="z_rows%d" % b) for b in range(HALVES)]
+        g_rows = [sb.tile([P, H], BF16, name="g_rows%d" % b) for b in range(HALVES)]
 
-        def in_word_order(turned):
-            return turned.rearrange("v (p u e) -> v u p e", u=2, e=2)
+        def fetch_centres(c, b, slot, turned):
+            nc.vector.tensor_copy(slot, h[c][:].indirect(cen_t[:, b * 8 : (b + 1) * 8]))
+            nc.tensor.transpose(turned, slot, ident[:])
+
+        def turn_back(rows, bk):
+            words = bank(bk, [P, 2, P])
+            pairs = rows[:].bitcast(F32)
+            for u in range(2):
+                nc.tensor.transpose(words[:, u, :], pairs[:, u : 2 * P : 2], ident[:])
+            return words
+
+        def interleave(words, name, copy):
+            values = sb.tile([P, P * PACK], BF16, name=name, align_bytes=64)
+            copy(
+                out=values[:].bitcast(F32).rearrange("p (v u) -> p v u", u=2),
+                in_=words[:].rearrange("p u v -> p v u"),
+            )
+            return values
+
+        def quantize(values, name):
+            codes = sb.tile([P, P], U32, name=name + "_codes", align_bytes=64)
+            scales = sb.tile([P, P], U8, name=name + "_scales", align_bytes=64)
+            nc.vector.quantize_mx(out=codes[:].bitcast(FP8X4), scales=scales[:], in_=values[:])
+            return codes, scales
+
+        def last_pass(acc, i, operand):
+            nc.tensor.matmul_mx(
+                out=acc[:],
+                lhsT=last_words[i][:].bitcast(FP8X4),
+                lhsT_scale=last_scales[i][:],
+                rhs=operand[0][:].bitcast(FP8X4),
+                rhs_scale=operand[1][:],
+                start=(i == 0),
+                stop=(i == 1),
+            )
+
+        def store(acc, b, copy):
+            result = sb.tile([P, P], F32, name="result%d" % b)
+            copy(result[:], acc[:])
+            nc.sync.dma_start(out=out[:, b * P : (b + 1) * P], in_=result[:])
 
         def sum_neighbours(chunks, banks):
             turned = [bank(bk, [P, len(chunks) * P]) for bk in banks]
@@ -150,90 +188,48 @@ def tile_picked_sagecat_mean_p_kernel(
                             start=(d == 0),
                             stop=(d == 2),
                         )
-                if c < 2:
-                    f = sb.tile([P, V], F32, name="centre%d" % c)
-                    nc.vector.tensor_copy(f[:], h[c][:].indirect(cen_t[:]))
-                    for b in range(HALVES):
-                        nc.tensor.transpose(g_early[:, b, c * P : (c + 1) * P], f[:, b * P : (b + 1) * P], ident[:])
-                if c == 1:
-                    for b in range(HALVES):
-                        nc.scalar.copy(out=g_rows[b][:, :, 0:64, :], in_=in_word_order(g_early[:, b, :]))
+                if c < CHUNKS - 1:
+                    fetch_centres(c, 0, centres[:, c * P : (c + 1) * P], g_first[:, c * P : (c + 1) * P])
             for b in range(HALVES):
                 nc.scalar.activation(
-                    out=z_rows[b][:, :, 32 * chunks.start : 32 * chunks.stop, :],
-                    in_=in_word_order(turned[b][:]),
+                    out=z_rows[b][:, P * chunks.start : P * chunks.stop],
+                    in_=turned[b][:],
                     func=COPY,
                     scale=1.0 / 3.0,
                 )
 
         fetched = {}
-        g_early = bank(5, [P, HALVES, 2 * P])
+        centres = sb.tile([P, H], F32, name="centres")
+        g_first = bank(5, [P, H])
         sum_neighbours(range(0, 3), (3, 4))
+        fetch_centres(3, 0, centres[:, 3 * P :], g_first[:, 3 * P :])
+        nc.scalar.copy(out=g_rows[0][:], in_=g_first[:])
+        g_values0 = interleave(turn_back(g_rows[0], 7), "g_values0", nc.scalar.copy)
         sum_neighbours(range(3, 4), (2, 6))
 
-        def fetch_centres(b, chunks, bk):
-            g_turned = bank(bk, [P, len(chunks) * P])
-            for i, c in enumerate(chunks):
-                slot = fetched[CHUNKS - 1, b][:, (c - 2) * P : (c - 1) * P]
-                nc.vector.tensor_copy(slot, h[c][:].indirect(cen_t[:, b * 8 : (b + 1) * 8]))
-                nc.tensor.transpose(g_turned[:, i * P : (i + 1) * P], slot, ident[:])
-            nc.scalar.copy(out=g_rows[b][:, :, 32 * chunks.start : 32 * chunks.stop, :], in_=in_word_order(g_turned[:]))
-
-        def turn_back(rows, words):
-            pairs = rows[:].rearrange("v u p e -> v (u p e)").bitcast(F32)
-            for u in range(2):
-                nc.tensor.transpose(words[:, u, :], pairs[:, u * P : (u + 1) * P], ident[:])
-
-        def centre_values(b, bk):
-            g_words = bank(bk, [P, 2, P])
-            turn_back(g_rows[b], g_words)
-            gb = sb.tile([P, P * PACK], BF16, name="g_bf%d" % b, align_bytes=64)
-            nc.scalar.copy(
-                out=gb[:].bitcast(F32).rearrange("p (v u) -> p v u", u=2),
-                in_=g_words[:].rearrange("p u v -> p v u"),
-            )
-            return gb
-
-        fetch_centres(0, range(2, 4), 0)
-        z_words = bank(5, [P, HALVES, 2, P])
-        for b in range(HALVES):
-            turn_back(z_rows[b], z_words[:, b])
-        z_bf = sb.tile([P, V * PACK], BF16, name="z_bf", align_bytes=64)
-        nc.scalar.copy(
-            out=z_bf[:].bitcast(F32).rearrange("p (b v u) -> p b v u", b=HALVES, u=2),
-            in_=z_words[:].rearrange("p b u v -> p b v u"),
-        )
-        z_codes = sb.tile([P, V], U32, name="z_codes", align_bytes=64)
-        z_scales = sb.tile([P, V], U8, name="z_scales", align_bytes=64)
-        fetch_centres(1, range(2, 3), 1)
-        fetch_centres(1, range(3, 4), 7)
-        g_bf = [centre_values(0, 3), centre_values(1, 4)]
-
-        nc.vector.quantize_mx(out=z_codes[:].bitcast(FP8X4), scales=z_scales[:], in_=z_bf[:])
-        for b in range(HALVES):
-            cols = slice(b * P, (b + 1) * P)
-            g_codes = sb.tile([P, P], U32, name="g_codes%d" % b, align_bytes=64)
-            g_scales = sb.tile([P, P], U8, name="g_scales%d" % b, align_bytes=64)
-            nc.vector.quantize_mx(out=g_codes[:].bitcast(FP8X4), scales=g_scales[:], in_=g_bf[b][:])
-            acc = bank((2, 6)[b], [P, P])
-            nc.tensor.matmul_mx(
-                out=acc[:],
-                lhsT=last_words[0][:].bitcast(FP8X4),
-                lhsT_scale=last_scales[0][:],
-                rhs=z_codes[:, cols].bitcast(FP8X4),
-                rhs_scale=z_scales[:, cols],
-                start=True,
-                stop=False,
-            )
-            nc.tensor.matmul_mx(
-                out=acc[:],
-                lhsT=last_words[1][:].bitcast(FP8X4),
-                lhsT_scale=last_scales[1][:],
-                rhs=g_codes[:].bitcast(FP8X4),
-                rhs_scale=g_scales[:],
-                start=False,
-                stop=True,
-            )
-            result = sb.tile([P, P], F32, name="result%d" % b)
-            nc.vector.tensor_copy(result[:], acc[:])
-            nc.sync.dma_start(out=out[:, cols], in_=result[:])
+        slots = [fetched[3, d][:, b * P : (b + 1) * P] for d in range(2) for b in range(HALVES)]
+        g_second = bank(0, [P, 3 * P])
+        g_last = bank(1, [P, P])
+        fetch_centres(0, 1, slots[0], g_second[:, 0:P])
+        fetch_centres(1, 1, slots[1], g_second[:, P : 2 * P])
+        z_words0 = turn_back(z_rows[0], 5)
+        fetch_centres(2, 1, slots[2], g_second[:, 2 * P :])
+        fetch_centres(3, 1, slots[3], g_last[:])
+        z_words1 = turn_back(z_rows[1], 2)
+        z_values0 = interleave(z_words0, "z_values0", nc.scalar.copy)
+        nc.scalar.copy(out=g_rows[1][:, : 3 * P], in_=g_second[:])
+        g0 = quantize(g_values0, "g0")
+        nc.vector.tensor_copy(out=g_rows[1][:, 3 * P :], in_=g_last[:])
+        z_values1 = interleave(z_words1, "z_values1", nc.scalar.copy)
+        g_words1 = turn_back(g_rows[1], 3)
+        z0 = quantize(z_values0, "z0")
+        acc0 = bank(4, [P, P])
+        last_pass(acc0, 0, z0)
+        last_pass(acc0, 1, g0)
+        z1 = quantize(z_values1, "z1")
+        acc1 = bank(7, [P, P])
+        last_pass(acc1, 0, z1)
+        g_values1 = interleave(g_words1, "g_values1", nc.vector.tensor_copy)
+        store(acc0, 0, nc.scalar.copy)
+        last_pass(acc1, 1, quantize(g_values1, "g1"))
+        store(acc1, 1, nc.vector.tensor_copy)

@@ -46,16 +46,11 @@ def tile_picked_sagecat_mean_p_kernel(
         offs_t = sb.tile([P, S // 16], U16, name="offs_t")
         nc.sync.dma_start(offs_t[:], offs)
         xs = sb.tile([P, T], U8, name="xs", align_bytes=64)
-        load_scales((nc.sync, nc.scalar, nc.scalar, nc.scalar), xs, x_scales)
+        load_scales((nc.sync, nc.scalar, nc.sync, nc.scalar), xs, x_scales)
         xw = sb.tile([P, T], I32, name="xw", align_bytes=64)
-        w1_rows = w1.rearrange("(p j) n -> p j n", j=PACK)
-        w1_raw = []
-        for c in range(CHUNKS):
-            raw = sb.tile([P, PACK, P], F32, name="w1_raw%d" % c)
-            nc.sync.dma_start(out=raw[:], in_=w1_rows[:, :, c * P : (c + 1) * P])
-            w1_raw.append(raw)
-            if c == 0:
-                nc.sync.dma_start(out=xw[:], in_=x_words[0].rearrange("p n t -> p (n t)").bitcast(I32))
+        w1_raw = sb.tile([P, PACK, H], F32, name="w1_raw")
+        nc.sync.dma_start(out=w1_raw[:], in_=w1.rearrange("(p j) n -> p j n", j=PACK))
+        nc.sync.dma_start(out=xw[:], in_=x_words[0].rearrange("p n t -> p (n t)").bitcast(I32))
         pos_t = []
         for d, pos in enumerate((pos1, pos2, pos3)):
             t = sb.tile([P, V // 16], U16, name="pos_t%d" % d)
@@ -76,23 +71,23 @@ def tile_picked_sagecat_mean_p_kernel(
         ident = sb.tile([P, P], F32, name="ident")
         make_identity(nc, ident[:])
 
-        w1_bf = {}
+        w1_bf = [sb.tile([P, 2, P, PACK], BF16, name="w1_bf%d" % u, align_bytes=64) for u in range(2)]
         w1_codes = [sb.tile([P, P], U32, name="w1_codes%d" % c, align_bytes=64) for c in range(CHUNKS)]
         w1_scales = [sb.tile([P, P], U8, name="w1_scales%d" % c, align_bytes=64) for c in range(CHUNKS)]
 
-        def round_w1(c):
-            w1_bf[c] = sb.tile([P, P, PACK], BF16, name="w1_bf%d" % min(c, 1), align_bytes=64)
-            nc.scalar.activation(
-                out=w1_bf[c][:].rearrange("p (n i) j -> p n j i", i=4),
-                in_=w1_raw[c][:].rearrange("p j (n i) -> p n j i", i=4),
-                func=COPY,
-            )
+        def round_w1(u, rows, on_vector):
+            dst = w1_bf[u][:].rearrange("p e m j -> p m e j")[:, rows]
+            src = w1_raw[:].rearrange("p j (m t) -> p m t j", t=PACK)[:, rows, 2 * u : 2 * u + 2, :]
+            if on_vector:
+                nc.vector.tensor_copy(out=dst, in_=src)
+            else:
+                nc.scalar.activation(out=dst, in_=src, func=COPY)
 
         def quantize_w1(c):
             nc.vector.quantize_mx(
                 out=w1_codes[c][:].bitcast(FP8X4),
                 scales=w1_scales[c][:],
-                in_=w1_bf[c][:].rearrange("p n j -> p (n j)"),
+                in_=w1_bf[c // 2][:, c % 2].rearrange("p m j -> p (m j)"),
             )
 
         picked_scales = sb.tile([P, S], U8, name="picked_scales", align_bytes=64)
@@ -116,31 +111,18 @@ def tile_picked_sagecat_mean_p_kernel(
                 nc.scalar.activation(out=h[c][:, cols], in_=acc[:], func=RELU)
 
         nc.vector.tensor_copy(picked_scales[:], xs[:].indirect(offs_t[:]))
-        round_w1(0)
+        round_w1(0, slice(0, 80), True)
+        round_w1(0, slice(80, P), False)
+        round_w1(1, slice(0, P), False)
         quantize_w1(0)
         for b, cols in enumerate((slice(0, 256), slice(256, 384), slice(384, 512))):
             nc.vector.tensor_copy(
                 picked_words[:, cols], xw[:].bitcast(U32).indirect(offs_t[:, cols.start // 16 : cols.stop // 16])
             )
             first_layer(0, b, cols, on_vector=(b == 2))
-        for c, b in ((1, 6), (2, 0), (3, 1)):
-            round_w1(c)
+        for c, b in ((1, 5), (2, 0), (3, 1)):
             quantize_w1(c)
             first_layer(c, b, slice(0, S))
-
-        z_rows = [sb.tile([P, H], BF16, name="z_rows%d" % b) for b in range(HALVES)]
-        g_rows = [sb.tile([P, H], BF16, name="g_rows%d" % b) for b in range(HALVES)]
-
-        def fetch_centres(c, b, slot, turned):
-            nc.vector.tensor_copy(slot, h[c][:].indirect(cen_t[:, b * 8 : (b + 1) * 8]))
-            nc.tensor.transpose(turned, slot, ident[:])
-
-        def turn_back(rows, bk):
-            words = bank(bk, [P, 2, P])
-            pairs = rows[:].bitcast(F32)
-            for u in range(2):
-                nc.tensor.transpose(words[:, u, :], pairs[:, u : 2 * P : 2], ident[:])
-            return words
 
         def interleave(words, name, copy):
             values = sb.tile([P, P * PACK], BF16, name=name, align_bytes=64)
@@ -153,7 +135,7 @@ def tile_picked_sagecat_mean_p_kernel(
         def quantize(values, name):
             codes = sb.tile([P, P], U32, name=name + "_codes", align_bytes=64)
             scales = sb.tile([P, P], U8, name=name + "_scales", align_bytes=64)
-            nc.vector.quantize_mx(out=codes[:].bitcast(FP8X4), scales=scales[:], in_=values[:])
+            nc.vector.quantize_mx(out=codes[:].bitcast(FP8X4), scales=scales[:], in_=values)
             return codes, scales
 
         def last_pass(acc, i, operand):
@@ -172,64 +154,52 @@ def tile_picked_sagecat_mean_p_kernel(
             copy(result[:], acc[:])
             nc.sync.dma_start(out=out[:, b * P : (b + 1) * P], in_=result[:])
 
-        def sum_neighbours(chunks, banks):
-            turned = [bank(bk, [P, len(chunks) * P]) for bk in banks]
-            for i, c in enumerate(chunks):
+        z_words = [bank(bk, [P, 2, P]) for bk in (7, 2)]
+        late = sb.tile([P, 2 * V], F32, name="late")
+        for u, banks in enumerate(((3, 4), (5, 6))):
+            turned = [bank(bk, [P, 2, P]) for bk in banks]
+            for e in range(2):
+                t = 2 * u + e
                 for d in range(3):
-                    f = sb.tile([P, V], F32, name="fetched%d_%d" % (c, d))
-                    fetched[c, d] = f
-                    nc.vector.tensor_copy(f[:], h[c][:].indirect(pos_t[d][:]))
+                    if t == 3 and d < 2:
+                        f = late[:, d * V : (d + 1) * V]
+                    else:
+                        f = sb.tile([P, V], F32, name="fetched%d_%d" % (t, d), align_bytes=64)[:]
+                    nc.vector.tensor_copy(f, h[t][:].indirect(pos_t[d][:]))
                     for b in range(HALVES):
                         nc.tensor.matmul(
-                            turned[b][:, i * P : (i + 1) * P],
+                            turned[b][:, e, :],
                             lhsT=f[:, b * P : (b + 1) * P],
                             rhs=ident[:],
                             is_transpose=True,
                             start=(d == 0),
                             stop=(d == 2),
                         )
-                if c < CHUNKS - 1:
-                    fetch_centres(c, 0, centres[:, c * P : (c + 1) * P], g_first[:, c * P : (c + 1) * P])
             for b in range(HALVES):
+                rows = sb.tile([P, P, 2], BF16, name="z_rows%d_%d" % (u, b))
                 nc.scalar.activation(
-                    out=z_rows[b][:, P * chunks.start : P * chunks.stop],
-                    in_=turned[b][:],
-                    func=COPY,
-                    scale=1.0 / 3.0,
+                    out=rows[:], in_=turned[b][:].rearrange("v e p -> v p e"), func=COPY, scale=1.0 / 3.0
                 )
+                nc.tensor.transpose(z_words[b][:, u, :], rows[:].rearrange("v p e -> v (p e)").bitcast(F32), ident[:])
 
-        fetched = {}
-        centres = sb.tile([P, H], F32, name="centres")
-        g_first = bank(5, [P, H])
-        sum_neighbours(range(0, 3), (3, 4))
-        fetch_centres(3, 0, centres[:, 3 * P :], g_first[:, 3 * P :])
-        nc.scalar.copy(out=g_rows[0][:], in_=g_first[:])
-        g_values0 = interleave(turn_back(g_rows[0], 7), "g_values0", nc.scalar.copy)
-        sum_neighbours(range(3, 4), (2, 6))
-
-        slots = [fetched[3, d][:, b * P : (b + 1) * P] for d in range(2) for b in range(HALVES)]
-        g_second = bank(0, [P, 3 * P])
-        g_last = bank(1, [P, P])
-        fetch_centres(0, 1, slots[0], g_second[:, 0:P])
-        fetch_centres(1, 1, slots[1], g_second[:, P : 2 * P])
-        z_words0 = turn_back(z_rows[0], 5)
-        fetch_centres(2, 1, slots[2], g_second[:, 2 * P :])
-        fetch_centres(3, 1, slots[3], g_last[:])
-        z_words1 = turn_back(z_rows[1], 2)
-        z_values0 = interleave(z_words0, "z_values0", nc.scalar.copy)
-        nc.scalar.copy(out=g_rows[1][:, : 3 * P], in_=g_second[:])
-        g0 = quantize(g_values0, "g0")
-        nc.vector.tensor_copy(out=g_rows[1][:, 3 * P :], in_=g_last[:])
-        z_values1 = interleave(z_words1, "z_values1", nc.scalar.copy)
-        g_words1 = turn_back(g_rows[1], 3)
-        z0 = quantize(z_values0, "z0")
-        acc0 = bank(4, [P, P])
+        for t in range(PACK):
+            nc.vector.tensor_copy(late[:, t * P : (t + 1) * P], h[t][:].indirect(cen_t[:, 0:8]))
+        g_values0 = sb.tile([P, P, PACK], BF16, name="g_values0", align_bytes=64)
+        nc.scalar.copy(out=g_values0[:], in_=late[:].rearrange("p (t v) -> p v t", t=PACK))
+        z_values0 = interleave(z_words[0], "z_values0", nc.scalar.copy)
+        z_values1 = interleave(z_words[1], "z_values1", nc.scalar.copy)
+        g_values1 = sb.tile([P, P, PACK], BF16, name="fetched3_2", align_bytes=64)
+        for t in range(PACK):
+            nc.vector.tensor_copy(g_values1[:, :, t], h[t][:].indirect(cen_t[:, 8:16]))
+        g0 = quantize(g_values0[:].rearrange("p v t -> p (v t)"), "g0")
+        z0 = quantize(z_values0[:], "z0")
+        acc0 = bank(3, [P, P])
         last_pass(acc0, 0, z0)
         last_pass(acc0, 1, g0)
-        z1 = quantize(z_values1, "z1")
-        acc1 = bank(7, [P, P])
+        g1 = quantize(g_values1[:].rearrange("p v t -> p (v t)"), "g1")
+        z1 = quantize(z_values1[:], "z1")
+        acc1 = bank(4, [P, P])
         last_pass(acc1, 0, z1)
-        g_values1 = interleave(g_words1, "g_values1", nc.vector.tensor_copy)
+        last_pass(acc1, 1, g1)
         store(acc0, 0, nc.scalar.copy)
-        last_pass(acc1, 1, quantize(g_values1, "g1"))
         store(acc1, 1, nc.vector.tensor_copy)

@@ -43,13 +43,18 @@ def tile_picked_sagecat_mean_p_kernel(
         def bank(b, shape):
             return ps.tile(shape, F32, name="bank%d" % b)
 
+        warm = sb.tile([P, 2], F32, name="warm")
+        nc.gpsimd.memset(warm[:, 0:1], 0.0)
+        nc.scalar.activation(out=warm[:, 1:2], in_=warm[:, 0:1], func=COPY)
+        w1_raw = sb.tile([P, PACK, H], F32, name="w1_raw")
+        w1_rows = w1.rearrange("(p j) n -> p j n", j=PACK)
+        nc.sync.dma_start(out=w1_raw[:, :1, :], in_=w1_rows[:, :1, :])
         offs_t = sb.tile([P, S // 16], U16, name="offs_t")
         nc.sync.dma_start(offs_t[:], offs)
         xs = sb.tile([P, T], U8, name="xs", align_bytes=64)
-        load_scales((nc.sync, nc.scalar, nc.sync, nc.scalar), xs, x_scales)
+        load_scales((nc.sync,) * 4, xs, x_scales)
         xw = sb.tile([P, T], I32, name="xw", align_bytes=64)
-        w1_raw = sb.tile([P, PACK, H], F32, name="w1_raw")
-        nc.sync.dma_start(out=w1_raw[:], in_=w1.rearrange("(p j) n -> p j n", j=PACK))
+        nc.sync.dma_start(out=w1_raw[:, 1:, :], in_=w1_rows[:, 1:, :])
         nc.sync.dma_start(out=xw[:], in_=x_words[0].rearrange("p n t -> p (n t)").bitcast(I32))
         pos_t = []
         for d, pos in enumerate((pos1, pos2, pos3)):
@@ -60,7 +65,7 @@ def tile_picked_sagecat_mean_p_kernel(
         nc.sync.dma_start(cen_t[:], cen)
         last_words = []
         last_scales = []
-        for i, (words, scales) in enumerate(((w3_words, w3_scales), (w2_words, w2_scales))):
+        for i, (words, scales) in enumerate(((w2_words, w2_scales), (w3_words, w3_scales))):
             wt = sb.tile([P, N], I32, name="last_words%d" % i, align_bytes=64)
             nc.sync.dma_start(out=wt[:], in_=words[0].rearrange("p n t -> p (n t)").bitcast(I32))
             st = sb.tile([P, N], U8, name="last_scales%d" % i, align_bytes=64)
@@ -132,8 +137,8 @@ def tile_picked_sagecat_mean_p_kernel(
             )
             return values
 
-        def quantize(values, name):
-            codes = sb.tile([P, P], U32, name=name + "_codes", align_bytes=64)
+        def quantize(values, name, codes_name=None):
+            codes = sb.tile([P, P], U32, name=codes_name or name + "_codes", align_bytes=64)
             scales = sb.tile([P, P], U8, name=name + "_scales", align_bytes=64)
             nc.vector.quantize_mx(out=codes[:].bitcast(FP8X4), scales=scales[:], in_=values)
             return codes, scales
@@ -149,13 +154,13 @@ def tile_picked_sagecat_mean_p_kernel(
                 stop=(i == 1),
             )
 
-        def store(acc, b, copy):
+        def store(acc, b, copy, queue):
             result = sb.tile([P, P], F32, name="result%d" % b)
             copy(result[:], acc[:])
-            nc.sync.dma_start(out=out[:, b * P : (b + 1) * P], in_=result[:])
+            queue.dma_start(out=out[:, b * P : (b + 1) * P], in_=result[:])
 
         z_words = [bank(bk, [P, 2, P]) for bk in (7, 2)]
-        late = sb.tile([P, 2 * V], F32, name="late")
+        late = sb.tile([P, 2 * V], F32, name="late", align_bytes=64)
         for u, banks in enumerate(((3, 4), (5, 6))):
             turned = [bank(bk, [P, 2, P]) for bk in banks]
             for e in range(2):
@@ -191,15 +196,10 @@ def tile_picked_sagecat_mean_p_kernel(
         g_values1 = sb.tile([P, P, PACK], BF16, name="fetched3_2", align_bytes=64)
         for t in range(PACK):
             nc.vector.tensor_copy(g_values1[:, :, t], h[t][:].indirect(cen_t[:, 8:16]))
-        g0 = quantize(g_values0[:].rearrange("p v t -> p (v t)"), "g0")
-        z0 = quantize(z_values0[:], "z0")
-        acc0 = bank(3, [P, P])
-        last_pass(acc0, 0, z0)
-        last_pass(acc0, 1, g0)
-        g1 = quantize(g_values1[:].rearrange("p v t -> p (v t)"), "g1")
-        z1 = quantize(z_values1[:], "z1")
-        acc1 = bank(4, [P, P])
-        last_pass(acc1, 0, z1)
-        last_pass(acc1, 1, g1)
-        store(acc0, 0, nc.scalar.copy)
-        store(acc1, 1, nc.vector.tensor_copy)
+        acc = [bank(3 + b, [P, P]) for b in range(HALVES)]
+        last_pass(acc[0], 0, quantize(g_values0[:].rearrange("p v t -> p (v t)"), "g0"))
+        last_pass(acc[1], 0, quantize(g_values1[:].rearrange("p v t -> p (v t)"), "g1", "late"))
+        last_pass(acc[0], 1, quantize(z_values0[:], "z0"))
+        last_pass(acc[1], 1, quantize(z_values1[:], "z1"))
+        store(acc[0], 0, nc.scalar.copy, nc.scalar)
+        store(acc[1], 1, nc.vector.tensor_copy, nc.sync)

@@ -32,6 +32,12 @@ def load_scales(queues, plane, scales):
         )
 
 
+def load_scale_rows(queue, plane, scales):
+    rows = scales[0].bitcast(I32)
+    for q in range(4):
+        queue.dma_start(out=plane[32 * q : 32 * q + 4, :].bitcast(I32), in_=rows[4 * q : 4 * q + 4, :])
+
+
 def tile_picked_sagecat_mean_p_kernel(
     tc, x_words, x_scales, w1, w2_words, w2_scales, w3_words, w3_scales, offs, cen, pos1, pos2, pos3, out
 ):
@@ -46,16 +52,19 @@ def tile_picked_sagecat_mean_p_kernel(
         warm = sb.tile([P, 2], F32, name="warm")
         nc.gpsimd.memset(warm[:, 0:1], 0.0)
         nc.scalar.activation(out=warm[:, 1:2], in_=warm[:, 0:1], func=COPY)
-        w1_raw = sb.tile([P, PACK, H], F32, name="w1_raw")
-        w1_rows = w1.rearrange("(p j) n -> p j n", j=PACK)
-        nc.sync.dma_start(out=w1_raw[:, :1, :], in_=w1_rows[:, :1, :])
         offs_t = sb.tile([P, S // 16], U16, name="offs_t")
         nc.sync.dma_start(offs_t[:], offs)
         xs = sb.tile([P, T], U8, name="xs", align_bytes=64)
-        load_scales((nc.sync,) * 4, xs, x_scales)
+        nc.vector.memset(xs[:].bitcast(I32), 0)
         xw = sb.tile([P, T], I32, name="xw", align_bytes=64)
-        nc.sync.dma_start(out=w1_raw[:, 1:, :], in_=w1_rows[:, 1:, :])
         nc.sync.dma_start(out=xw[:], in_=x_words[0].rearrange("p n t -> p (n t)").bitcast(I32))
+        load_scale_rows(nc.sync, xs, x_scales)
+        w1_rows = w1.rearrange("(p j) n -> p j n", j=PACK)
+        w1_raw = []
+        for a in range(2):
+            raw = sb.tile([P, 2, H], F32, name="w1_raw%d" % a)
+            nc.sync.dma_start(out=raw[:], in_=w1_rows[:, 2 * a : 2 * a + 2, :])
+            w1_raw.append(raw)
         pos_t = []
         for d, pos in enumerate((pos1, pos2, pos3)):
             t = sb.tile([P, V // 16], U16, name="pos_t%d" % d)
@@ -80,9 +89,11 @@ def tile_picked_sagecat_mean_p_kernel(
         w1_codes = [sb.tile([P, P], U32, name="w1_codes%d" % c, align_bytes=64) for c in range(CHUNKS)]
         w1_scales = [sb.tile([P, P], U8, name="w1_scales%d" % c, align_bytes=64) for c in range(CHUNKS)]
 
-        def round_w1(u, rows, on_vector):
-            dst = w1_bf[u][:].rearrange("p e m j -> p m e j")[:, rows]
-            src = w1_raw[:].rearrange("p j (m t) -> p m t j", t=PACK)[:, rows, 2 * u : 2 * u + 2, :]
+        def round_w1(a, u, planes, on_vector):
+            dst = w1_bf[u][:].rearrange("p e m j -> p m e j")[:, :, planes, 2 * a : 2 * a + 2]
+            src = w1_raw[a][:].rearrange("p j (m t) -> p m t j", t=PACK)[
+                :, :, 2 * u + planes.start : 2 * u + planes.stop, :
+            ]
             if on_vector:
                 nc.vector.tensor_copy(out=dst, in_=src)
             else:
@@ -115,17 +126,19 @@ def tile_picked_sagecat_mean_p_kernel(
             else:
                 nc.scalar.activation(out=h[c][:, cols], in_=acc[:], func=RELU)
 
+        nc.vector.tensor_copy(picked_words[:], xw[:].bitcast(U32).indirect(offs_t[:]))
         nc.vector.tensor_copy(picked_scales[:], xs[:].indirect(offs_t[:]))
-        round_w1(0, slice(0, 80), True)
-        round_w1(0, slice(80, P), False)
-        round_w1(1, slice(0, P), False)
+        round_w1(0, 0, slice(0, 2), False)
+        round_w1(0, 1, slice(0, 2), False)
+        round_w1(1, 0, slice(0, 1), True)
         quantize_w1(0)
-        for b, cols in enumerate((slice(0, 256), slice(256, 384), slice(384, 512))):
-            nc.vector.tensor_copy(
-                picked_words[:, cols], xw[:].bitcast(U32).indirect(offs_t[:, cols.start // 16 : cols.stop // 16])
-            )
-            first_layer(0, b, cols, on_vector=(b == 2))
-        for c, b in ((1, 5), (2, 0), (3, 1)):
+        round_w1(1, 0, slice(1, 2), True)
+        round_w1(1, 1, slice(0, 2), False)
+        for b in range(4):
+            first_layer(0, b, slice(b * P, (b + 1) * P))
+        quantize_w1(1)
+        first_layer(1, 5, slice(0, S))
+        for c, b in ((2, 0), (3, 1)):
             quantize_w1(c)
             first_layer(c, b, slice(0, S))
 

@@ -52,12 +52,12 @@ def tile_picked_sagecat_mean_p_kernel(
         warm = sb.tile([P, 2], F32, name="warm")
         nc.gpsimd.memset(warm[:, 0:1], 0.0)
         nc.scalar.activation(out=warm[:, 1:2], in_=warm[:, 0:1], func=COPY)
-        offs_t = sb.tile([P, S // 16], U16, name="offs_t")
-        nc.sync.dma_start(offs_t[:], offs)
         xs = sb.tile([P, T], U8, name="xs", align_bytes=64)
         nc.vector.memset(xs[:].bitcast(I32), 0)
         xw = sb.tile([P, T], I32, name="xw", align_bytes=64)
         nc.sync.dma_start(out=xw[:], in_=x_words[0].rearrange("p n t -> p (n t)").bitcast(I32))
+        offs_t = sb.tile([P, S // 16], U16, name="offs_t")
+        nc.sync.dma_start(offs_t[:], offs)
         load_scale_rows(nc.sync, xs, x_scales)
         w1_rows = w1.rearrange("(p j) n -> p j n", j=PACK)
         w1_raw = []
@@ -108,7 +108,7 @@ def tile_picked_sagecat_mean_p_kernel(
 
         picked_scales = sb.tile([P, S], U8, name="picked_scales", align_bytes=64)
         picked_words = sb.tile([P, S], U32, name="picked_words", align_bytes=64)
-        h = [sb.tile([P, S], F32, name="h%d" % c) for c in range(CHUNKS)]
+        h = [sb.tile([P, S], F32, name="h%d" % c, align_bytes=64) for c in range(CHUNKS)]
 
         def first_layer(c, b, cols, on_vector=False):
             acc = bank(b, [P, cols.stop - cols.start])
@@ -150,21 +150,20 @@ def tile_picked_sagecat_mean_p_kernel(
             )
             return values
 
-        def quantize(values, name, codes_name=None):
-            codes = sb.tile([P, P], U32, name=codes_name or name + "_codes", align_bytes=64)
+        def quantize(values, name, codes):
             scales = sb.tile([P, P], U8, name=name + "_scales", align_bytes=64)
-            nc.vector.quantize_mx(out=codes[:].bitcast(FP8X4), scales=scales[:], in_=values)
+            nc.vector.quantize_mx(out=codes.bitcast(FP8X4), scales=scales[:], in_=values)
             return codes, scales
 
-        def last_pass(acc, i, operand):
+        def last_pass(acc, i, operand, first):
             nc.tensor.matmul_mx(
                 out=acc[:],
                 lhsT=last_words[i][:].bitcast(FP8X4),
                 lhsT_scale=last_scales[i][:],
-                rhs=operand[0][:].bitcast(FP8X4),
+                rhs=operand[0].bitcast(FP8X4),
                 rhs_scale=operand[1][:],
-                start=(i == 0),
-                stop=(i == 1),
+                start=first,
+                stop=not first,
             )
 
         def store(acc, b, copy, queue):
@@ -173,18 +172,24 @@ def tile_picked_sagecat_mean_p_kernel(
             queue.dma_start(out=out[:, b * P : (b + 1) * P], in_=result[:])
 
         z_words = [bank(bk, [P, 2, P]) for bk in (7, 2)]
-        late = sb.tile([P, 2 * V], F32, name="late", align_bytes=64)
+        late = sb.tile([P, PACK * V], F32, name="late", align_bytes=64)
         for u, banks in enumerate(((3, 4), (5, 6))):
             turned = [bank(bk, [P, 2, P]) for bk in banks]
             for e in range(2):
                 t = 2 * u + e
                 for d in range(3):
-                    if t == 3 and d < 2:
+                    if t == 3:
                         f = late[:, d * V : (d + 1) * V]
                     else:
                         f = sb.tile([P, V], F32, name="fetched%d_%d" % (t, d), align_bytes=64)[:]
-                    nc.vector.tensor_copy(f, h[t][:].indirect(pos_t[d][:]))
+                    last = (t, d) == (3, 2)
+                    if not last:
+                        nc.vector.tensor_copy(f, h[t][:].indirect(pos_t[d][:]))
                     for b in range(HALVES):
+                        if last:
+                            nc.vector.tensor_copy(
+                                f[:, b * P : (b + 1) * P], h[t][:].indirect(pos_t[d][:, 8 * b : 8 * b + 8])
+                            )
                         nc.tensor.matmul(
                             turned[b][:, e, :],
                             lhsT=f[:, b * P : (b + 1) * P],
@@ -194,25 +199,32 @@ def tile_picked_sagecat_mean_p_kernel(
                             stop=(d == 2),
                         )
             for b in range(HALVES):
-                rows = sb.tile([P, P, 2], BF16, name="z_rows%d_%d" % (u, b))
+                if u == 1:
+                    rows = late[:, 3 * V + b * P : 3 * V + (b + 1) * P].bitcast(BF16).rearrange("v (p e) -> v p e", e=2)
+                else:
+                    rows = sb.tile([P, P, 2], BF16, name="z_rows%d_%d" % (u, b))[:]
                 nc.scalar.activation(
-                    out=rows[:], in_=turned[b][:].rearrange("v e p -> v p e"), func=COPY, scale=1.0 / 3.0
+                    out=rows, in_=turned[b][:].rearrange("v e p -> v p e"), func=COPY, scale=1.0 / 3.0
                 )
-                nc.tensor.transpose(z_words[b][:, u, :], rows[:].rearrange("v p e -> v (p e)").bitcast(F32), ident[:])
+                nc.tensor.transpose(z_words[b][:, u, :], rows.rearrange("v p e -> v (p e)").bitcast(F32), ident[:])
 
-        for t in range(PACK):
-            nc.vector.tensor_copy(late[:, t * P : (t + 1) * P], h[t][:].indirect(cen_t[:, 0:8]))
-        g_values0 = sb.tile([P, P, PACK], BF16, name="g_values0", align_bytes=64)
-        nc.scalar.copy(out=g_values0[:], in_=late[:].rearrange("p (t v) -> p v t", t=PACK))
-        z_values0 = interleave(z_words[0], "z_values0", nc.scalar.copy)
-        z_values1 = interleave(z_words[1], "z_values1", nc.scalar.copy)
-        g_values1 = sb.tile([P, P, PACK], BF16, name="fetched3_2", align_bytes=64)
-        for t in range(PACK):
-            nc.vector.tensor_copy(g_values1[:, :, t], h[t][:].indirect(cen_t[:, 8:16]))
+        z_values = [interleave(z_words[b], "z_values%d" % b, nc.scalar.copy) for b in range(HALVES)]
+        for t in range(PACK - 1):
+            nc.vector.tensor_copy(late[:, t * V : (t + 1) * V], h[t][:].indirect(cen_t[:]))
+        for b in range(HALVES):
+            nc.vector.tensor_copy(
+                late[:, 3 * V + b * P : 3 * V + (b + 1) * P], h[3][:].indirect(cen_t[:, 8 * b : 8 * b + 8])
+            )
+        centres = late[:].rearrange("p (t v) -> p v t", t=PACK)
+        g_values = [sb.tile([P, P, PACK], BF16, name="g_values%d" % b, align_bytes=64) for b in range(HALVES)]
+        g_codes = [sb.tile([P, P], U32, name="g_codes%d" % b, align_bytes=64) for b in range(HALVES)]
+        z_codes = sb.tile([P, V], U32, name="h3", align_bytes=64)
         acc = [bank(3 + b, [P, P]) for b in range(HALVES)]
-        last_pass(acc[0], 0, quantize(g_values0[:].rearrange("p v t -> p (v t)"), "g0"))
-        last_pass(acc[1], 0, quantize(g_values1[:].rearrange("p v t -> p (v t)"), "g1", "late"))
-        last_pass(acc[0], 1, quantize(z_values0[:], "z0"))
-        last_pass(acc[1], 1, quantize(z_values1[:], "z1"))
-        store(acc[0], 0, nc.scalar.copy, nc.scalar)
-        store(acc[1], 1, nc.vector.tensor_copy, nc.sync)
+        nc.scalar.copy(out=g_values[0][:], in_=centres[:, :P])
+        last_pass(acc[0], 1, quantize(z_values[0][:], "z0", z_codes[:, :P]), True)
+        nc.vector.tensor_copy(out=g_values[1][:], in_=centres[:, P:])
+        last_pass(acc[1], 1, quantize(z_values[1][:], "z1", z_codes[:, P:]), True)
+        for b in (1, 0):
+            last_pass(acc[b], 0, quantize(g_values[b][:].rearrange("p v t -> p (v t)"), "g%d" % b, g_codes[b][:]), False)
+        store(acc[1], 1, nc.scalar.copy, nc.scalar)
+        store(acc[0], 0, nc.vector.tensor_copy, nc.sync)

@@ -18,24 +18,34 @@ RELU = mybir.ActivationFunctionType.Relu
 
 P = 128
 PACK = 4
-CHUNKS = H // P
 HALVES = V // P
+NEIGHBOURS = 3
+PER_COLUMN = 16
+VECTOR_ROWS = 72
 
 
-def load_scales(queues, plane, scales):
-    width = scales.shape[2]
-    rows = scales.bitcast(I32)
-    for q, queue in enumerate(queues):
-        queue.dma_start(
-            out=plane[32 * q : 32 * q + 32, :].bitcast(I32),
-            in_=rows[:, 4 * q : 4 * q + 4, :].broadcast_to([8, 4, width // 4]),
-        )
+def load_words(nc, tile, words):
+    nc.sync.dma_start(out=tile[:], in_=words[0].rearrange("p n t -> p (n t)").bitcast(I32))
 
 
-def load_scale_rows(queue, plane, scales):
+def load_scales(nc, rows_out, scales):
     rows = scales[0].bitcast(I32)
     for q in range(4):
-        queue.dma_start(out=plane[32 * q : 32 * q + 4, :].bitcast(I32), in_=rows[4 * q : 4 * q + 4, :])
+        nc.sync.dma_start(out=rows_out[32 * q : 32 * q + 4].bitcast(I32), in_=rows[4 * q : 4 * q + 4])
+
+
+def load_list(nc, pool, entries, name):
+    tile = pool.tile(list(entries.shape), U16, name=name)
+    nc.sync.dma_start(tile[:], entries)
+    return tile
+
+
+def half(b):
+    return slice(b * P, (b + 1) * P)
+
+
+def list_half(tile, b):
+    return tile[:, b * P // PER_COLUMN : (b + 1) * P // PER_COLUMN]
 
 
 def tile_picked_sagecat_mean_p_kernel(
@@ -46,185 +56,149 @@ def tile_picked_sagecat_mean_p_kernel(
         sb = ctx.enter_context(tc.tile_pool(name="sb", bufs=1))
         ps = ctx.enter_context(tc.psum_pool(name="ps", bufs=1))
 
-        def bank(b, shape):
-            return ps.tile(shape, F32, name="bank%d" % b)
+        def bank(number, shape):
+            return ps.tile(shape, F32, name="bank%d" % number)
 
-        warm = sb.tile([P, 2], F32, name="warm")
-        nc.gpsimd.memset(warm[:, 0:1], 0.0)
-        nc.scalar.activation(out=warm[:, 1:2], in_=warm[:, 0:1], func=COPY)
-        xs = sb.tile([P, T], U8, name="xs", align_bytes=64)
-        nc.vector.memset(xs[:].bitcast(I32), 0)
-        xw = sb.tile([P, T], I32, name="xw", align_bytes=64)
-        nc.sync.dma_start(out=xw[:], in_=x_words[0].rearrange("p n t -> p (n t)").bitcast(I32))
-        offs_t = sb.tile([P, S // 16], U16, name="offs_t")
-        nc.sync.dma_start(offs_t[:], offs)
-        load_scale_rows(nc.sync, xs, x_scales)
-        w1_rows = w1.rearrange("(p j) n -> p j n", j=PACK)
-        w1_raw = []
-        for a in range(2):
-            raw = sb.tile([P, 2, H], F32, name="w1_raw%d" % a)
-            nc.sync.dma_start(out=raw[:], in_=w1_rows[:, 2 * a : 2 * a + 2, :])
-            w1_raw.append(raw)
-        pos_t = []
-        for d, pos in enumerate((pos1, pos2, pos3)):
-            t = sb.tile([P, V // 16], U16, name="pos_t%d" % d)
-            nc.sync.dma_start(t[:], pos)
-            pos_t.append(t)
-        cen_t = sb.tile([P, V // 16], U16, name="cen_t")
-        nc.sync.dma_start(cen_t[:], cen)
-        last_words = []
-        last_scales = []
+        x_scale_tile = sb.tile([P, T], U8, name="x_scale_tile", align_bytes=64)
+        nc.vector.memset(x_scale_tile[:].bitcast(I32), 0)
+        last_scales = sb.tile([P, 2 * N], U8, name="last_scales", align_bytes=64)
+        nc.vector.memset(last_scales[:].bitcast(I32), 0)
+
+        x_word_tile = sb.tile([P, T], I32, name="x_word_tile", align_bytes=64)
+        load_words(nc, x_word_tile, x_words)
+        offs_tile = load_list(nc, sb, offs, "offs_tile")
+        load_scales(nc, x_scale_tile, x_scales)
+        w1_raw = sb.tile([P, PACK, H], F32, name="w1_raw")
+        nc.sync.dma_start(out=w1_raw[:], in_=w1.rearrange("(p j) c -> p j c", j=PACK))
+        pos_tiles = [load_list(nc, sb, pos, "pos_tile%d" % d) for d, pos in enumerate((pos1, pos2, pos3))]
+        cen_tile = load_list(nc, sb, cen, "cen_tile")
+        last_weights = []
         for i, (words, scales) in enumerate(((w2_words, w2_scales), (w3_words, w3_scales))):
-            wt = sb.tile([P, N], I32, name="last_words%d" % i, align_bytes=64)
-            nc.sync.dma_start(out=wt[:], in_=words[0].rearrange("p n t -> p (n t)").bitcast(I32))
-            st = sb.tile([P, N], U8, name="last_scales%d" % i, align_bytes=64)
-            load_scales((nc.sync,) * 4, st, scales)
-            last_words.append(wt)
-            last_scales.append(st)
+            word_tile = sb.tile([P, N], I32, name="last_words%d" % i, align_bytes=64)
+            load_words(nc, word_tile, words)
+            scale_columns = last_scales[:, i * N : (i + 1) * N]
+            load_scales(nc, scale_columns, scales)
+            last_weights.append((word_tile[:], scale_columns))
+        w2, w3 = last_weights
 
         ident = sb.tile([P, P], F32, name="ident")
         make_identity(nc, ident[:])
 
-        w1_bf = [sb.tile([P, 2, P, PACK], BF16, name="w1_bf%d" % u, align_bytes=64) for u in range(2)]
-        w1_codes = [sb.tile([P, P], U32, name="w1_codes%d" % c, align_bytes=64) for c in range(CHUNKS)]
-        w1_scales = [sb.tile([P, P], U8, name="w1_scales%d" % c, align_bytes=64) for c in range(CHUNKS)]
-
-        def round_w1(a, u, planes, on_vector):
-            dst = w1_bf[u][:].rearrange("p e m j -> p m e j")[:, :, planes, 2 * a : 2 * a + 2]
-            src = w1_raw[a][:].rearrange("p j (m t) -> p m t j", t=PACK)[
-                :, :, 2 * u + planes.start : 2 * u + planes.stop, :
-            ]
-            if on_vector:
-                nc.vector.tensor_copy(out=dst, in_=src)
-            else:
-                nc.scalar.activation(out=dst, in_=src, func=COPY)
-
-        def quantize_w1(c):
-            nc.vector.quantize_mx(
-                out=w1_codes[c][:].bitcast(FP8X4),
-                scales=w1_scales[c][:],
-                in_=w1_bf[c // 2][:, c % 2].rearrange("p m j -> p (m j)"),
-            )
-
-        picked_scales = sb.tile([P, S], U8, name="picked_scales", align_bytes=64)
-        picked_words = sb.tile([P, S], U32, name="picked_words", align_bytes=64)
-        h = [sb.tile([P, S], F32, name="h%d" % c, align_bytes=64) for c in range(CHUNKS)]
-
-        def first_layer(c, b, cols, on_vector=False):
-            acc = bank(b, [P, cols.stop - cols.start])
-            nc.tensor.matmul_mx(
-                out=acc[:],
-                lhsT=w1_codes[c][:].bitcast(FP8X4),
-                lhsT_scale=w1_scales[c][:],
-                rhs=picked_words[:, cols].bitcast(FP8X4),
-                rhs_scale=picked_scales[:, cols],
-                start=True,
-                stop=True,
-            )
-            if on_vector:
-                nc.vector.tensor_scalar_max(h[c][:, cols], acc[:], 0.0)
-            else:
-                nc.scalar.activation(out=h[c][:, cols], in_=acc[:], func=RELU)
-
-        nc.vector.tensor_copy(picked_words[:], xw[:].bitcast(U32).indirect(offs_t[:]))
-        nc.vector.tensor_copy(picked_scales[:], xs[:].indirect(offs_t[:]))
-        round_w1(0, 0, slice(0, 2), False)
-        round_w1(0, 1, slice(0, 2), False)
-        round_w1(1, 0, slice(0, 1), True)
-        quantize_w1(0)
-        round_w1(1, 0, slice(1, 2), True)
-        round_w1(1, 1, slice(0, 2), False)
-        for b in range(4):
-            first_layer(0, b, slice(b * P, (b + 1) * P))
-        quantize_w1(1)
-        first_layer(1, 5, slice(0, S))
-        for c, b in ((2, 0), (3, 1)):
-            quantize_w1(c)
-            first_layer(c, b, slice(0, S))
-
-        def interleave(words, name, copy):
-            values = sb.tile([P, P * PACK], BF16, name=name, align_bytes=64)
-            copy(
-                out=values[:].bitcast(F32).rearrange("p (v u) -> p v u", u=2),
-                in_=words[:].rearrange("p u v -> p v u"),
-            )
-            return values
-
-        def quantize(values, name, codes):
+        def quantize(values, codes, name):
             scales = sb.tile([P, P], U8, name=name + "_scales", align_bytes=64)
             nc.vector.quantize_mx(out=codes.bitcast(FP8X4), scales=scales[:], in_=values)
-            return codes, scales
+            return codes, scales[:]
 
-        def last_pass(acc, i, operand, first):
+        def mx_pass(acc, stationary, moving, start, stop):
             nc.tensor.matmul_mx(
-                out=acc[:],
-                lhsT=last_words[i][:].bitcast(FP8X4),
-                lhsT_scale=last_scales[i][:],
-                rhs=operand[0].bitcast(FP8X4),
-                rhs_scale=operand[1][:],
-                start=first,
-                stop=not first,
+                out=acc,
+                lhsT=stationary[0].bitcast(FP8X4),
+                lhsT_scale=stationary[1],
+                rhs=moving[0].bitcast(FP8X4),
+                rhs_scale=moving[1],
+                start=start,
+                stop=stop,
             )
 
-        def store(acc, b, copy, queue):
-            result = sb.tile([P, P], F32, name="result%d" % b)
-            copy(result[:], acc[:])
-            queue.dma_start(out=out[:, b * P : (b + 1) * P], in_=result[:])
+        picked_words = sb.tile([P, S], U32, name="picked_words", align_bytes=64)
+        picked_scales = sb.tile([P, S], U8, name="picked_scales", align_bytes=64)
+        nc.vector.tensor_copy(picked_words[:], x_word_tile[:].bitcast(U32).indirect(offs_tile[:]))
+        nc.vector.tensor_copy(picked_scales[:], x_scale_tile[:].indirect(offs_tile[:]))
 
-        z_words = [bank(bk, [P, 2, P]) for bk in (7, 2)]
+        def round_w1(u):
+            rounded = sb.tile([P, 2, P, PACK], BF16, name="w1_rounded%d" % u, align_bytes=64)
+            dst = rounded[:].rearrange("p e m j -> p m e j")
+            src = w1_raw[:].rearrange("p j (m t) -> p m t j", t=PACK)[:, :, 2 * u : 2 * u + 2, :]
+            nc.vector.tensor_copy(out=dst[:, :VECTOR_ROWS], in_=src[:, :VECTOR_ROWS])
+            nc.scalar.activation(out=dst[:, VECTOR_ROWS:], in_=src[:, VECTOR_ROWS:], func=COPY)
+            return rounded
+
+        h = [sb.tile([P, S], F32, name="h%d" % t, align_bytes=64) for t in range(PACK)]
+
+        def make_plane(t, rounded, banks):
+            codes = sb.tile([P, P], U32, name="w1_codes%d" % t, align_bytes=64)
+            weights = quantize(rounded[:, t % 2].rearrange("p m j -> p (m j)"), codes[:], "w1_%d" % t)
+            width = S // len(banks)
+            for piece, number in enumerate(banks):
+                entries = slice(piece * width, (piece + 1) * width)
+                acc = bank(number, [P, width])
+                mx_pass(acc[:], weights, (picked_words[:, entries], picked_scales[:, entries]), True, True)
+                nc.scalar.activation(out=h[t][:, entries], in_=acc[:], func=RELU)
+
+        plane_banks = ((0, 1, 2, 3), (5,), (0,), (1,))
+        for u in range(2):
+            rounded = round_w1(u)
+            for t in (2 * u, 2 * u + 1):
+                make_plane(t, rounded, plane_banks[t])
+
         late = sb.tile([P, PACK * V], F32, name="late", align_bytes=64)
-        for u, banks in enumerate(((3, 4), (5, 6))):
-            turned = [bank(bk, [P, 2, P]) for bk in banks]
+
+        def late_half(t, b):
+            return late[:, t * V : (t + 1) * V][:, half(b)]
+
+        z_words = [bank(number, [P, 2, P]) for number in (7, 2)]
+        for u, sum_banks in enumerate(((3, 4), (5, 6))):
+            turned = [bank(number, [P, 2, P]) for number in sum_banks]
             for e in range(2):
                 t = 2 * u + e
-                for d in range(3):
-                    if t == 3:
-                        f = late[:, d * V : (d + 1) * V]
+                for d in range(NEIGHBOURS):
+                    if t == PACK - 1:
+                        fetched = late[:, d * V : (d + 1) * V]
                     else:
-                        f = sb.tile([P, V], F32, name="fetched%d_%d" % (t, d), align_bytes=64)[:]
-                    last = (t, d) == (3, 2)
-                    if not last:
-                        nc.vector.tensor_copy(f, h[t][:].indirect(pos_t[d][:]))
+                        fetched = sb.tile([P, V], F32, name="fetched%d_%d" % (t, d), align_bytes=64)[:]
+                    by_halves = (t, d) == (PACK - 1, NEIGHBOURS - 1)
+                    if not by_halves:
+                        nc.vector.tensor_copy(fetched, h[t][:].indirect(pos_tiles[d][:]))
                     for b in range(HALVES):
-                        if last:
-                            nc.vector.tensor_copy(
-                                f[:, b * P : (b + 1) * P], h[t][:].indirect(pos_t[d][:, 8 * b : 8 * b + 8])
-                            )
+                        if by_halves:
+                            nc.vector.tensor_copy(fetched[:, half(b)], h[t][:].indirect(list_half(pos_tiles[d], b)))
                         nc.tensor.matmul(
                             turned[b][:, e, :],
-                            lhsT=f[:, b * P : (b + 1) * P],
+                            lhsT=fetched[:, half(b)],
                             rhs=ident[:],
                             is_transpose=True,
                             start=(d == 0),
-                            stop=(d == 2),
+                            stop=(d == NEIGHBOURS - 1),
                         )
             for b in range(HALVES):
                 if u == 1:
-                    rows = late[:, 3 * V + b * P : 3 * V + (b + 1) * P].bitcast(BF16).rearrange("v (p e) -> v p e", e=2)
+                    pairs = late_half(PACK - 1, b)
                 else:
-                    rows = sb.tile([P, P, 2], BF16, name="z_rows%d_%d" % (u, b))[:]
+                    pairs = sb.tile([P, P], F32, name="pairs%d" % b)[:]
                 nc.scalar.activation(
-                    out=rows, in_=turned[b][:].rearrange("v e p -> v p e"), func=COPY, scale=1.0 / 3.0
+                    out=pairs.bitcast(BF16).rearrange("v (p e) -> v p e", e=2),
+                    in_=turned[b][:].rearrange("v e p -> v p e"),
+                    func=COPY,
+                    scale=1.0 / NEIGHBOURS,
                 )
-                nc.tensor.transpose(z_words[b][:, u, :], rows.rearrange("v p e -> v (p e)").bitcast(F32), ident[:])
+                nc.tensor.transpose(z_words[b][:, u, :], pairs, ident[:])
 
-        z_values = [interleave(z_words[b], "z_values%d" % b, nc.scalar.copy) for b in range(HALVES)]
-        for t in range(PACK - 1):
-            nc.vector.tensor_copy(late[:, t * V : (t + 1) * V], h[t][:].indirect(cen_t[:]))
+        z_values = []
         for b in range(HALVES):
-            nc.vector.tensor_copy(
-                late[:, 3 * V + b * P : 3 * V + (b + 1) * P], h[3][:].indirect(cen_t[:, 8 * b : 8 * b + 8])
+            values = sb.tile([P, P * PACK], BF16, name="z_values%d" % b, align_bytes=64)
+            nc.scalar.copy(
+                out=values[:].bitcast(F32).rearrange("p (v u) -> p v u", u=2),
+                in_=z_words[b][:].rearrange("p u v -> p v u"),
             )
+            z_values.append(values)
+
+        for t in range(PACK - 1):
+            nc.vector.tensor_copy(late[:, t * V : (t + 1) * V], h[t][:].indirect(cen_tile[:]))
+        for b in range(HALVES):
+            nc.vector.tensor_copy(late_half(PACK - 1, b), h[PACK - 1][:].indirect(list_half(cen_tile, b)))
         centres = late[:].rearrange("p (t v) -> p v t", t=PACK)
+
         g_values = [sb.tile([P, P, PACK], BF16, name="g_values%d" % b, align_bytes=64) for b in range(HALVES)]
         g_codes = [sb.tile([P, P], U32, name="g_codes%d" % b, align_bytes=64) for b in range(HALVES)]
-        z_codes = sb.tile([P, V], U32, name="h3", align_bytes=64)
-        acc = [bank(3 + b, [P, P]) for b in range(HALVES)]
-        nc.scalar.copy(out=g_values[0][:], in_=centres[:, :P])
-        last_pass(acc[0], 1, quantize(z_values[0][:], "z0", z_codes[:, :P]), True)
-        nc.vector.tensor_copy(out=g_values[1][:], in_=centres[:, P:])
-        last_pass(acc[1], 1, quantize(z_values[1][:], "z1", z_codes[:, P:]), True)
+        z_codes = sb.tile([P, V], U32, name="h%d" % (PACK - 1), align_bytes=64)
+        groups = [bank(number, [P, P]) for number in (3, 4)]
+        for b, copy in enumerate((nc.scalar.copy, nc.vector.tensor_copy)):
+            copy(out=g_values[b][:], in_=centres[:, half(b)])
+            mx_pass(groups[b][:], w3, quantize(z_values[b][:], z_codes[:, half(b)], "z%d" % b), True, False)
         for b in (1, 0):
-            last_pass(acc[b], 0, quantize(g_values[b][:].rearrange("p v t -> p (v t)"), "g%d" % b, g_codes[b][:]), False)
-        store(acc[1], 1, nc.scalar.copy, nc.scalar)
-        store(acc[0], 0, nc.vector.tensor_copy, nc.sync)
+            g = quantize(g_values[b][:].rearrange("p v t -> p (v t)"), g_codes[b][:], "g%d" % b)
+            mx_pass(groups[b][:], w2, g, False, True)
+        for b, copy, queue in ((1, nc.scalar.copy, nc.scalar), (0, nc.vector.tensor_copy, nc.sync)):
+            result = sb.tile([P, P], F32, name="result%d" % b)
+            copy(result[:], groups[b][:])
+            queue.dma_start(out=out[:, half(b)], in_=result[:])

@@ -21,7 +21,6 @@ PACK = 4
 HALVES = V // P
 NEIGHBOURS = 3
 PER_COLUMN = 16
-VECTOR_ROWS = 72
 
 
 def load_words(nc, tile, words):
@@ -68,8 +67,12 @@ def tile_picked_sagecat_mean_p_kernel(
         load_words(nc, x_word_tile, x_words)
         offs_tile = load_list(nc, sb, offs, "offs_tile")
         load_scales(nc, x_scale_tile, x_scales)
-        w1_raw = sb.tile([P, PACK, H], F32, name="w1_raw")
-        nc.sync.dma_start(out=w1_raw[:], in_=w1.rearrange("(p j) c -> p j c", j=PACK))
+        w1_rows = w1.rearrange("(p a j) c -> a p j c", a=2, j=2)
+        w1_raw = []
+        for a in range(2):
+            raw = sb.tile([P, 2, H], F32, name="w1_raw%d" % a)
+            nc.sync.dma_start(out=raw[:], in_=w1_rows[a])
+            w1_raw.append(raw)
         pos_tiles = [load_list(nc, sb, pos, "pos_tile%d" % d) for d, pos in enumerate((pos1, pos2, pos3))]
         cen_tile = load_list(nc, sb, cen, "cen_tile")
         last_weights = []
@@ -105,19 +108,22 @@ def tile_picked_sagecat_mean_p_kernel(
         nc.vector.tensor_copy(picked_words[:], x_word_tile[:].bitcast(U32).indirect(offs_tile[:]))
         nc.vector.tensor_copy(picked_scales[:], x_scale_tile[:].indirect(offs_tile[:]))
 
-        def round_w1(u):
-            rounded = sb.tile([P, 2, P, PACK], BF16, name="w1_rounded%d" % u, align_bytes=64)
-            dst = rounded[:].rearrange("p e m j -> p m e j")
-            src = w1_raw[:].rearrange("p j (m t) -> p m t j", t=PACK)[:, :, 2 * u : 2 * u + 2, :]
-            nc.vector.tensor_copy(out=dst[:, :VECTOR_ROWS], in_=src[:, :VECTOR_ROWS])
-            nc.scalar.activation(out=dst[:, VECTOR_ROWS:], in_=src[:, VECTOR_ROWS:], func=COPY)
-            return rounded
+        rounded = [sb.tile([P, 2, P, PACK], BF16, name="w1_rounded%d" % u, align_bytes=64) for u in range(2)]
+
+        def rounding(a, first, count):
+            dst = rounded[first // 2][:].rearrange("p e m j -> p m e j")
+            src = w1_raw[a][:].rearrange("p j (m t) -> p m t j", t=PACK)
+            return dict(
+                out=dst[:, :, first % 2 : first % 2 + count, 2 * a : 2 * a + 2], in_=src[:, :, first : first + count]
+            )
+
+        def quantize_w1(t):
+            codes = sb.tile([P, P], U32, name="w1_codes%d" % t, align_bytes=64)
+            return quantize(rounded[t // 2][:, t % 2].rearrange("p m j -> p (m j)"), codes[:], "w1_%d" % t)
 
         h = [sb.tile([P, S], F32, name="h%d" % t, align_bytes=64) for t in range(PACK)]
 
-        def make_plane(t, rounded, banks):
-            codes = sb.tile([P, P], U32, name="w1_codes%d" % t, align_bytes=64)
-            weights = quantize(rounded[:, t % 2].rearrange("p m j -> p (m j)"), codes[:], "w1_%d" % t)
+        def make_plane(t, weights, banks):
             width = S // len(banks)
             for piece, number in enumerate(banks):
                 entries = slice(piece * width, (piece + 1) * width)
@@ -125,11 +131,15 @@ def tile_picked_sagecat_mean_p_kernel(
                 mx_pass(acc[:], weights, (picked_words[:, entries], picked_scales[:, entries]), True, True)
                 nc.scalar.activation(out=h[t][:, entries], in_=acc[:], func=RELU)
 
-        plane_banks = ((0, 1, 2, 3), (5,), (0,), (1,))
-        for u in range(2):
-            rounded = round_w1(u)
-            for t in (2 * u, 2 * u + 1):
-                make_plane(t, rounded, plane_banks[t])
+        for first in (0, 2):
+            nc.scalar.activation(func=COPY, **rounding(0, first, 2))
+        nc.vector.tensor_copy(**rounding(1, 0, 1))
+        weights = quantize_w1(0)
+        nc.vector.tensor_copy(**rounding(1, 1, 1))
+        nc.scalar.activation(func=COPY, **rounding(1, 2, 2))
+        make_plane(0, weights, (0, 1, 2, 3))
+        for t, number in ((1, 5), (2, 0), (3, 1)):
+            make_plane(t, quantize_w1(t), (number,))
 
         late = sb.tile([P, PACK * V], F32, name="late", align_bytes=64)
 

@@ -1,7 +1,6 @@
 from contextlib import ExitStack
 
 import concourse.mybir as mybir
-from concourse.masks import make_identity
 
 K, T, S, V, H, N = 512, 1024, 512, 256, 512, 128
 FLOPS = 2 * K * H * S + 2 * 2 * H * N * V
@@ -15,6 +14,7 @@ U8 = mybir.dt.uint8
 FP8X4 = mybir.dt.float8_e4m3fn_x4
 COPY = mybir.ActivationFunctionType.Copy
 RELU = mybir.ActivationFunctionType.Relu
+ADD = mybir.AluOpType.add
 
 P = 128
 PACK = 4
@@ -84,9 +84,6 @@ def tile_picked_sagecat_mean_p_kernel(
             last_weights.append((word_tile[:], scale_columns))
         w2, w3 = last_weights
 
-        ident = sb.tile([P, P], F32, name="ident")
-        make_identity(nc, ident[:])
-
         def quantize(values, codes, name):
             scales = sb.tile([P, P], U8, name=name + "_scales", align_bytes=64)
             nc.vector.quantize_mx(out=codes.bitcast(FP8X4), scales=scales[:], in_=values)
@@ -138,77 +135,73 @@ def tile_picked_sagecat_mean_p_kernel(
         nc.vector.tensor_copy(**rounding(1, 1, 1))
         nc.scalar.activation(func=COPY, **rounding(1, 2, 2))
         make_plane(0, weights, (0, 1, 2, 3))
-        for t, number in ((1, 5), (2, 0), (3, 1)):
+        for t, number in ((1, 4), (2, 5), (3, 6)):
             make_plane(t, quantize_w1(t), (number,))
 
-        late = sb.tile([P, PACK * V], F32, name="late", align_bytes=64)
+        centres = [sb.tile([P, 2, V], F32, name="centres%d" % u, align_bytes=64) for u in range(2)]
+        first_sums = sb.tile([P, 2, V], F32, name="first_sums", align_bytes=64)
+        late = sb.tile([P, 2 * V - P + 2 * V], F32, name="late", align_bytes=64)
+        g_values = late[:, 2 * V - P :].bitcast(BF16)
+        sums = [first_sums[:], late[:, : 2 * V].rearrange("p (e v) -> p e v", e=2)]
+        z_values = [sb.tile([P, P, PACK], BF16, name="z_values%d" % b, align_bytes=64) for b in range(HALVES)]
+        g_codes = sb.tile([P, V], U32, name="g_codes", align_bytes=64)
+        g_scales = sb.tile([P, V], U8, name="g_scales", align_bytes=64)
 
-        def late_half(t, b):
-            return late[:, t * V : (t + 1) * V][:, half(b)]
+        def interleave(values, u, sums):
+            return values[:, :, 2 * u : 2 * u + 2], sums.rearrange("p e v -> p v e")
 
-        z_words = [bank(number, [P, 2, P]) for number in (7, 2)]
-        for u, sum_banks in enumerate(((3, 4), (5, 6))):
-            turned = [bank(number, [P, 2, P]) for number in sum_banks]
-            for e in range(2):
-                t = 2 * u + e
-                for d in range(NEIGHBOURS):
-                    if t == PACK - 1:
-                        fetched = late[:, d * V : (d + 1) * V]
-                    else:
-                        fetched = sb.tile([P, V], F32, name="fetched%d_%d" % (t, d), align_bytes=64)[:]
-                    by_halves = (t, d) == (PACK - 1, NEIGHBOURS - 1)
-                    if not by_halves:
-                        nc.vector.tensor_copy(fetched, h[t][:].indirect(pos_tiles[d][:]))
-                    for b in range(HALVES):
-                        if by_halves:
-                            nc.vector.tensor_copy(fetched[:, half(b)], h[t][:].indirect(list_half(pos_tiles[d], b)))
-                        nc.tensor.matmul(
-                            turned[b][:, e, :],
-                            lhsT=fetched[:, half(b)],
-                            rhs=ident[:],
-                            is_transpose=True,
-                            start=(d == 0),
-                            stop=(d == NEIGHBOURS - 1),
-                        )
+        def gather_centres(t):
+            nc.vector.tensor_copy(centres[t // 2][:, t % 2], h[t][:].indirect(cen_tile[:]))
+            if t % 2:
+                dst, src = interleave(g_values.rearrange("p (v t) -> p v t", t=PACK), t // 2, centres[t // 2][:])
+                nc.scalar.activation(out=dst, in_=src, func=COPY)
+
+        one = [sb.tile([P, V], F32, name="one%d" % t, align_bytes=64) for t in range(PACK)]
+        two = [sb.tile([P, V], F32, name="two%d" % t, align_bytes=64) for t in range(PACK)]
+
+        def neighbour(d, t, b=None):
+            targets = slice(0, V) if b is None else half(b)
+            fetched = h[t][:].indirect(pos_tiles[d][:] if b is None else list_half(pos_tiles[d], b))
+            if d == 0:
+                nc.vector.tensor_copy(one[t][:, targets], fetched)
+            elif d == 1:
+                nc.vector.tensor_tensor(two[t][:, targets], fetched, one[t][:, targets], ADD)
+            else:
+                nc.vector.tensor_tensor(sums[t // 2][:, t % 2, targets], fetched, two[t][:, targets], ADD)
+
+        last = PACK - 1
+        neighbour(0, 0)
+        for t in range(last):
+            gather_centres(t)
+            neighbour(1, t)
+            if t + 1 < last:
+                neighbour(0, t + 1)
+            else:
+                gather_centres(last)
+            neighbour(2, t)
+            if t == 1:
+                for b in range(HALVES):
+                    dst, src = interleave(z_values[b][:], 0, sums[0][:, :, half(b)])
+                    nc.scalar.activation(out=dst, in_=src, func=COPY, scale=1.0 / NEIGHBOURS)
+        for d in range(NEIGHBOURS):
             for b in range(HALVES):
-                if u == 1:
-                    pairs = late_half(PACK - 1, b)
-                else:
-                    pairs = sb.tile([P, P], F32, name="pairs%d" % b)[:]
-                nc.scalar.activation(
-                    out=pairs.bitcast(BF16).rearrange("v (p e) -> v p e", e=2),
-                    in_=turned[b][:].rearrange("v e p -> v p e"),
-                    func=COPY,
-                    scale=1.0 / NEIGHBOURS,
-                )
-                nc.tensor.transpose(z_words[b][:, u, :], pairs, ident[:])
+                if (d, b) == (NEIGHBOURS - 1, 1):
+                    nc.vector.quantize_mx(out=g_codes[:].bitcast(FP8X4), scales=g_scales[:], in_=g_values)
+                neighbour(d, last, b)
+        last_sums = [sums[1][:, :, half(b)] for b in range(HALVES)]
 
-        z_values = []
+        groups = [bank(number, [P, P]) for number in (7, 0)]
         for b in range(HALVES):
-            values = sb.tile([P, P * PACK], BF16, name="z_values%d" % b, align_bytes=64)
-            nc.scalar.copy(
-                out=values[:].bitcast(F32).rearrange("p (v u) -> p v u", u=2),
-                in_=z_words[b][:].rearrange("p u v -> p v u"),
-            )
-            z_values.append(values)
-
-        for t in range(PACK - 1):
-            nc.vector.tensor_copy(late[:, t * V : (t + 1) * V], h[t][:].indirect(cen_tile[:]))
-        for b in range(HALVES):
-            nc.vector.tensor_copy(late_half(PACK - 1, b), h[PACK - 1][:].indirect(list_half(cen_tile, b)))
-        centres = late[:].rearrange("p (t v) -> p v t", t=PACK)
-
-        g_values = [sb.tile([P, P, PACK], BF16, name="g_values%d" % b, align_bytes=64) for b in range(HALVES)]
-        g_codes = [sb.tile([P, P], U32, name="g_codes%d" % b, align_bytes=64) for b in range(HALVES)]
-        z_codes = sb.tile([P, V], U32, name="h%d" % (PACK - 1), align_bytes=64)
-        groups = [bank(number, [P, P]) for number in (3, 4)]
-        for b, copy in enumerate((nc.scalar.copy, nc.vector.tensor_copy)):
-            copy(out=g_values[b][:], in_=centres[:, half(b)])
-            mx_pass(groups[b][:], w3, quantize(z_values[b][:], z_codes[:, half(b)], "z%d" % b), True, False)
-        for b in (1, 0):
-            g = quantize(g_values[b][:].rearrange("p v t -> p (v t)"), g_codes[b][:], "g%d" % b)
-            mx_pass(groups[b][:], w2, g, False, True)
-        for b, copy, queue in ((1, nc.scalar.copy, nc.scalar), (0, nc.vector.tensor_copy, nc.sync)):
+            mx_pass(groups[b][:], w2, (g_codes[:, half(b)], g_scales[:, half(b)]), True, False)
+        dst, src = interleave(z_values[0][:], 1, last_sums[0])
+        nc.scalar.activation(out=dst, in_=src, func=COPY, scale=1.0 / NEIGHBOURS)
+        dst, src = interleave(z_values[1][:], 1, last_sums[1])
+        nc.vector.tensor_scalar_mul(dst, src, 1.0 / NEIGHBOURS)
+        for b, tag in enumerate(("z_codes0", "z_values0")):
+            codes = sb.tile([P, P], U32, name=tag, align_bytes=64)
+            z = quantize(z_values[b][:].rearrange("p v t -> p (v t)"), codes[:], "z%d" % b)
+            mx_pass(groups[b][:], w3, z, False, True)
+        for b, copy, queue in ((0, nc.scalar.copy, nc.scalar), (1, nc.vector.tensor_copy, nc.sync)):
             result = sb.tile([P, P], F32, name="result%d" % b)
             copy(result[:], groups[b][:])
             queue.dma_start(out=out[:, half(b)], in_=result[:])

@@ -139,10 +139,8 @@ def tile_picked_sagecat_mean_p_kernel(
             make_plane(t, quantize_w1(t), (number,))
 
         centres = [sb.tile([P, 2, V], F32, name="centres%d" % u, align_bytes=64) for u in range(2)]
-        first_sums = sb.tile([P, 2, V], F32, name="first_sums", align_bytes=64)
-        late = sb.tile([P, 2 * V - P + 2 * V], F32, name="late", align_bytes=64)
-        g_values = late[:, 2 * V - P :].bitcast(BF16)
-        sums = [first_sums[:], late[:, : 2 * V].rearrange("p (e v) -> p e v", e=2)]
+        sums = [sb.tile([P, 2, V], F32, name="sums%d" % u, align_bytes=64) for u in range(2)]
+        g_values = sb.tile([P, V * PACK], BF16, name="g_values", align_bytes=64)[:]
         z_values = [sb.tile([P, P, PACK], BF16, name="z_values%d" % b, align_bytes=64) for b in range(HALVES)]
         g_codes = sb.tile([P, V], U32, name="g_codes", align_bytes=64)
         g_scales = sb.tile([P, V], U8, name="g_scales", align_bytes=64)
@@ -178,6 +176,7 @@ def tile_picked_sagecat_mean_p_kernel(
                 neighbour(0, t + 1)
             else:
                 gather_centres(last)
+                nc.vector.quantize_mx(out=g_codes[:].bitcast(FP8X4), scales=g_scales[:], in_=g_values)
             neighbour(2, t)
             if t == 1:
                 for b in range(HALVES):
@@ -185,8 +184,6 @@ def tile_picked_sagecat_mean_p_kernel(
                     nc.scalar.activation(out=dst, in_=src, func=COPY, scale=1.0 / NEIGHBOURS)
         for d in range(NEIGHBOURS):
             for b in range(HALVES):
-                if (d, b) == (NEIGHBOURS - 1, 1):
-                    nc.vector.quantize_mx(out=g_codes[:].bitcast(FP8X4), scales=g_scales[:], in_=g_values)
                 neighbour(d, last, b)
         last_sums = [sums[1][:, :, half(b)] for b in range(HALVES)]
 
@@ -197,8 +194,8 @@ def tile_picked_sagecat_mean_p_kernel(
         nc.scalar.activation(out=dst, in_=src, func=COPY, scale=1.0 / NEIGHBOURS)
         dst, src = interleave(z_values[1][:], 1, last_sums[1])
         nc.vector.tensor_scalar_mul(dst, src, 1.0 / NEIGHBOURS)
-        for b, tag in enumerate(("z_codes0", "z_values0")):
-            codes = sb.tile([P, P], U32, name=tag, align_bytes=64)
+        for b in range(HALVES):
+            codes = sb.tile([P, P], U32, name="z_codes%d" % b, align_bytes=64)
             z = quantize(z_values[b][:].rearrange("p v t -> p (v t)"), codes[:], "z%d" % b)
             mx_pass(groups[b][:], w3, z, False, True)
         for b, copy, queue in ((0, nc.scalar.copy, nc.scalar), (1, nc.vector.tensor_copy, nc.sync)):

@@ -142,7 +142,6 @@ def tile_picked_sagecat_mean_p_kernel(
         sums = [sb.tile([P, 2, V], F32, name="sums%d" % u, align_bytes=64) for u in range(2)]
         g_values = sb.tile([P, V * PACK], BF16, name="g_values", align_bytes=64)[:]
         z_values = [sb.tile([P, P, PACK], BF16, name="z_values%d" % b, align_bytes=64) for b in range(HALVES)]
-        g_codes = sb.tile([P, V], U32, name="g_codes", align_bytes=64)
         g_scales = sb.tile([P, V], U8, name="g_scales", align_bytes=64)
 
         def interleave(values, u, sums):
@@ -167,24 +166,28 @@ def tile_picked_sagecat_mean_p_kernel(
             else:
                 nc.vector.tensor_tensor(sums[t // 2][:, t % 2, targets], fetched, two[t][:, targets], ADD)
 
-        last = PACK - 1
         neighbour(0, 0)
-        for t in range(last):
-            gather_centres(t)
-            neighbour(1, t)
-            if t + 1 < last:
-                neighbour(0, t + 1)
-            else:
-                gather_centres(last)
-                nc.vector.quantize_mx(out=g_codes[:].bitcast(FP8X4), scales=g_scales[:], in_=g_values)
-            neighbour(2, t)
-            if t == 1:
-                for b in range(HALVES):
-                    dst, src = interleave(z_values[b][:], 0, sums[0][:, :, half(b)])
-                    nc.scalar.activation(out=dst, in_=src, func=COPY, scale=1.0 / NEIGHBOURS)
-        for d in range(NEIGHBOURS):
-            for b in range(HALVES):
-                neighbour(d, last, b)
+        gather_centres(0)
+        neighbour(1, 0)
+        neighbour(0, 1)
+        neighbour(2, 0)
+        gather_centres(1)
+        neighbour(1, 1)
+        neighbour(0, 2)
+        neighbour(2, 1)
+        for b in range(HALVES):
+            dst, src = interleave(z_values[b][:], 0, sums[0][:, :, half(b)])
+            nc.scalar.activation(out=dst, in_=src, func=COPY, scale=1.0 / NEIGHBOURS)
+        gather_centres(2)
+        gather_centres(3)
+        neighbour(0, 3)
+        neighbour(1, 2)
+        neighbour(1, 3)
+        neighbour(2, 2)
+        for b in range(HALVES):
+            neighbour(2, 3, b)
+        g_codes = sb.tile([P, V], U32, name="two2", align_bytes=64)
+        nc.vector.quantize_mx(out=g_codes[:].bitcast(FP8X4), scales=g_scales[:], in_=g_values)
         last_sums = [sums[1][:, :, half(b)] for b in range(HALVES)]
 
         groups = [bank(number, [P, P]) for number in (7, 0)]

@@ -23,8 +23,8 @@ NEIGHBOURS = 3
 PER_COLUMN = 16
 
 
-def load_words(nc, tile, words):
-    nc.sync.dma_start(out=tile[:], in_=words[0].rearrange("p n t -> p (n t)").bitcast(I32))
+def load_words(queue, tile, words):
+    queue.dma_start(out=tile[:], in_=words[0].rearrange("p n t -> p (n t)").bitcast(I32))
 
 
 def load_scales(nc, rows_out, scales):
@@ -64,7 +64,7 @@ def tile_picked_sagecat_mean_p_kernel(
         nc.vector.memset(last_scales[:].bitcast(I32), 0)
 
         x_word_tile = sb.tile([P, T], I32, name="x_word_tile", align_bytes=64)
-        load_words(nc, x_word_tile, x_words)
+        load_words(nc.scalar, x_word_tile, x_words)
         offs_tile = load_list(nc, sb, offs, "offs_tile")
         load_scales(nc, x_scale_tile, x_scales)
         w1_rows = w1.rearrange("(p a j) c -> a p j c", a=2, j=2)
@@ -78,7 +78,7 @@ def tile_picked_sagecat_mean_p_kernel(
         last_weights = []
         for i, (words, scales) in enumerate(((w2_words, w2_scales), (w3_words, w3_scales))):
             word_tile = sb.tile([P, N], I32, name="last_words%d" % i, align_bytes=64)
-            load_words(nc, word_tile, words)
+            load_words(nc.sync, word_tile, words)
             scale_columns = last_scales[:, i * N : (i + 1) * N]
             load_scales(nc, scale_columns, scales)
             last_weights.append((word_tile[:], scale_columns))

@@ -120,88 +120,87 @@ def tile_picked_sagecat_mean_p_kernel(
 
         h = [sb.tile([P, S], F32, name="h%d" % t, align_bytes=64) for t in range(PACK)]
 
-        def make_plane(t, weights, banks):
+        def relu_scalar(dst, acc):
+            nc.scalar.activation(out=dst, in_=acc, func=RELU)
+
+        def relu_vector(dst, acc):
+            nc.vector.tensor_scalar_max(dst, acc, 0.0)
+
+        def make_plane(t, weights, banks, relu):
             width = S // len(banks)
             for piece, number in enumerate(banks):
                 entries = slice(piece * width, (piece + 1) * width)
                 acc = bank(number, [P, width])
                 mx_pass(acc[:], weights, (picked_words[:, entries], picked_scales[:, entries]), True, True)
-                nc.scalar.activation(out=h[t][:, entries], in_=acc[:], func=RELU)
+                relu(h[t][:, entries], acc[:])
 
         for first in (0, 2):
             nc.scalar.activation(func=COPY, **rounding(0, first, 2))
         nc.vector.tensor_copy(**rounding(1, 0, 1))
-        weights = quantize_w1(0)
+        weights0 = quantize_w1(0)
         nc.vector.tensor_copy(**rounding(1, 1, 1))
         nc.scalar.activation(func=COPY, **rounding(1, 2, 2))
-        make_plane(0, weights, (0, 1, 2, 3))
-        for t, number in ((1, 4), (2, 5), (3, 6)):
-            make_plane(t, quantize_w1(t), (number,))
+        make_plane(0, weights0, (0, 1, 2, 3), relu_scalar)
+        weights = [weights0] + [quantize_w1(t) for t in range(1, PACK)]
 
-        centres = [sb.tile([P, 2, V], F32, name="centres%d" % u, align_bytes=64) for u in range(2)]
-        sums = [sb.tile([P, 2, V], F32, name="sums%d" % u, align_bytes=64) for u in range(2)]
-        g_values = sb.tile([P, V * PACK], BF16, name="g_values", align_bytes=64)[:]
-        z_values = [sb.tile([P, P, PACK], BF16, name="z_values%d" % b, align_bytes=64) for b in range(HALVES)]
-        g_scales = sb.tile([P, V], U8, name="g_scales", align_bytes=64)
-
-        def interleave(values, u, sums):
-            return values[:, :, 2 * u : 2 * u + 2], sums.rearrange("p e v -> p v e")
-
-        def gather_centres(t):
-            nc.vector.tensor_copy(centres[t // 2][:, t % 2], h[t][:].indirect(cen_tile[:]))
-            if t % 2:
-                dst, src = interleave(g_values.rearrange("p (v t) -> p v t", t=PACK), t // 2, centres[t // 2][:])
-                nc.scalar.activation(out=dst, in_=src, func=COPY)
-
+        sums = sb.tile([P, PACK, V], F32, name="sums", align_bytes=64)
         one = [sb.tile([P, V], F32, name="one%d" % t, align_bytes=64) for t in range(PACK)]
         two = [sb.tile([P, V], F32, name="two%d" % t, align_bytes=64) for t in range(PACK)]
 
-        def neighbour(d, t, b=None):
+        def first_neighbour(t):
+            nc.scalar.activation(out=one[t][:], in_=h[t][:].indirect(pos_tiles[0][:]), func=COPY)
+
+        def second_neighbour(t):
+            nc.vector.tensor_tensor(two[t][:], h[t][:].indirect(pos_tiles[1][:]), one[t][:], ADD)
+
+        def third_neighbour(t, b=None):
             targets = slice(0, V) if b is None else half(b)
-            fetched = h[t][:].indirect(pos_tiles[d][:] if b is None else list_half(pos_tiles[d], b))
-            if d == 0:
-                nc.vector.tensor_copy(one[t][:, targets], fetched)
-            elif d == 1:
-                nc.vector.tensor_tensor(two[t][:, targets], fetched, one[t][:, targets], ADD)
-            else:
-                nc.vector.tensor_tensor(sums[t // 2][:, t % 2, targets], fetched, two[t][:, targets], ADD)
+            offsets = pos_tiles[2][:] if b is None else list_half(pos_tiles[2], b)
+            nc.vector.tensor_tensor(sums[:, t, targets], h[t][:].indirect(offsets), two[t][:, targets], ADD)
 
-        neighbour(0, 0)
-        gather_centres(0)
-        neighbour(1, 0)
-        neighbour(0, 1)
-        neighbour(2, 0)
-        gather_centres(1)
-        neighbour(1, 1)
-        neighbour(0, 2)
-        neighbour(2, 1)
-        for b in range(HALVES):
-            dst, src = interleave(z_values[b][:], 0, sums[0][:, :, half(b)])
-            nc.scalar.activation(out=dst, in_=src, func=COPY, scale=1.0 / NEIGHBOURS)
-        gather_centres(2)
-        gather_centres(3)
-        neighbour(0, 3)
-        neighbour(1, 2)
-        neighbour(1, 3)
-        neighbour(2, 2)
-        for b in range(HALVES):
-            neighbour(2, 3, b)
-        g_codes = sb.tile([P, V], U32, name="two2", align_bytes=64)
-        nc.vector.quantize_mx(out=g_codes[:].bitcast(FP8X4), scales=g_scales[:], in_=g_values)
-        last_sums = [sums[1][:, :, half(b)] for b in range(HALVES)]
+        def centre(t):
+            nc.scalar.activation(out=centres[:, t], in_=h[t][:].indirect(cen_tile[:]), func=COPY)
 
-        groups = [bank(number, [P, P]) for number in (7, 0)]
+        first_neighbour(0)
+        make_plane(1, weights[1], (4, 5), relu_vector)
+        second_neighbour(0)
+        first_neighbour(1)
+        make_plane(2, weights[2], (6,), relu_scalar)
+        make_plane(3, weights[3], (7,), relu_scalar)
+        second_neighbour(1)
+        third_neighbour(0)
+        third_neighbour(1)
+        for step in (first_neighbour, second_neighbour):
+            for t in (2, 3):
+                step(t)
+        third_neighbour(2)
         for b in range(HALVES):
-            mx_pass(groups[b][:], w2, (g_codes[:, half(b)], g_scales[:, half(b)]), True, False)
-        dst, src = interleave(z_values[0][:], 1, last_sums[0])
-        nc.scalar.activation(out=dst, in_=src, func=COPY, scale=1.0 / NEIGHBOURS)
-        dst, src = interleave(z_values[1][:], 1, last_sums[1])
-        nc.vector.tensor_scalar_mul(dst, src, 1.0 / NEIGHBOURS)
+            third_neighbour(3, b)
+        centres = sb.tile([P, PACK, V], BF16, name="two1", align_bytes=64)
+        for t in range(PACK):
+            centre(t)
+
+        z_values = sb.tile([P, V, PACK], BF16, name="z_values", align_bytes=64)
+        g_values = [sb.tile([P, P, PACK], BF16, name="g_values%d" % b, align_bytes=64) for b in range(HALVES)]
         for b in range(HALVES):
-            codes = sb.tile([P, P], U32, name="z_codes%d" % b, align_bytes=64)
-            z = quantize(z_values[b][:].rearrange("p v t -> p (v t)"), codes[:], "z%d" % b)
-            mx_pass(groups[b][:], w3, z, False, True)
-        for b, copy, queue in ((0, nc.scalar.copy, nc.scalar), (1, nc.vector.tensor_copy, nc.sync)):
+            nc.vector.tensor_scalar_mul(
+                z_values[:, half(b)], sums[:, :, half(b)].rearrange("p t v -> p v t"), 1.0 / NEIGHBOURS
+            )
+        z_codes = sb.tile([P, V], U32, name="z_codes", align_bytes=64)
+        z_scales = sb.tile([P, V], U8, name="z_scales", align_bytes=64)
+        nc.scalar.copy(g_values[1][:], centres[:, :, half(1)].rearrange("p t v -> p v t"))
+        nc.vector.tensor_copy(g_values[0][:], centres[:, :, half(0)].rearrange("p t v -> p v t"))
+        nc.vector.quantize_mx(
+            out=z_codes[:].bitcast(FP8X4), scales=z_scales[:], in_=z_values[:].rearrange("p v t -> p (v t)")
+        )
+        groups = [bank(number, [P, P]) for number in (0, 1)]
+        for b in range(HALVES):
+            mx_pass(groups[b][:], w3, (z_codes[:, half(b)], z_scales[:, half(b)]), True, False)
+        for b in (1, 0):
+            codes = sb.tile([P, P], U32, name="g_codes%d" % b, align_bytes=64)
+            g = quantize(g_values[b][:].rearrange("p v t -> p (v t)"), codes[:], "g%d" % b)
+            mx_pass(groups[b][:], w2, g, False, True)
+        for b, copy, queue in ((1, nc.scalar.copy, nc.scalar), (0, nc.vector.tensor_copy, nc.sync)):
             result = sb.tile([P, P], F32, name="result%d" % b)
             copy(result[:], groups[b][:])
             queue.dma_start(out=out[:, half(b)], in_=result[:])

@@ -115,10 +115,10 @@ def tile_picked_sagecat_mean_p_kernel(
             )
 
         def quantize_w1(t):
-            codes = sb.tile([P, P], U32, name="w1_codes%d" % t, align_bytes=64)
+            codes = sb.tile([P, P], U32, name="w1_codes%d" % (1 if t == 3 else t), align_bytes=64)
             return quantize(rounded[t // 2][:, t % 2].rearrange("p m j -> p (m j)"), codes[:], "w1_%d" % t)
 
-        h = [sb.tile([P, S], F32, name="h%d" % t, align_bytes=64) for t in range(PACK)]
+        h = {}
 
         def relu_scalar(dst, acc):
             nc.scalar.activation(out=dst, in_=acc, func=RELU)
@@ -128,6 +128,7 @@ def tile_picked_sagecat_mean_p_kernel(
 
         def make_plane(t, weights, banks, relu):
             width = S // len(banks)
+            h[t] = sb.tile([P, S], F32, name="w1_rounded1" if t == 2 else "h%d" % t, align_bytes=64)
             for piece, number in enumerate(banks):
                 entries = slice(piece * width, (piece + 1) * width)
                 acc = bank(number, [P, width])
@@ -141,13 +142,13 @@ def tile_picked_sagecat_mean_p_kernel(
         nc.vector.tensor_copy(**rounding(1, 1, 1))
         nc.scalar.activation(func=COPY, **rounding(1, 2, 2))
         make_plane(0, weights0, (0, 1, 2, 3), relu_scalar)
-        weights = [weights0] + [quantize_w1(t) for t in range(1, PACK)]
+        weights = [weights0] + [quantize_w1(t) for t in (1, 2)]
 
-        sums = sb.tile([P, PACK, V], F32, name="sums", align_bytes=64)
-        one = [sb.tile([P, V], F32, name="one%d" % t, align_bytes=64) for t in range(PACK)]
+        one = {}
         two = [sb.tile([P, V], F32, name="two%d" % t, align_bytes=64) for t in range(PACK)]
 
         def first_neighbour(t):
+            one[t] = sb.tile([P, V], F32, name="w1_codes1" if t == 2 else "one%d" % t, align_bytes=64)
             nc.scalar.activation(out=one[t][:], in_=h[t][:].indirect(pos_tiles[0][:]), func=COPY)
 
         def second_neighbour(t):
@@ -158,16 +159,20 @@ def tile_picked_sagecat_mean_p_kernel(
             offsets = pos_tiles[2][:] if b is None else list_half(pos_tiles[2], b)
             nc.vector.tensor_tensor(sums[:, t, targets], h[t][:].indirect(offsets), two[t][:, targets], ADD)
 
-        def centre(t):
-            nc.scalar.activation(out=centres[:, t], in_=h[t][:].indirect(cen_tile[:]), func=COPY)
+        def centre(t, b=None):
+            targets = slice(0, V) if b is None else half(b)
+            offsets = cen_tile[:] if b is None else list_half(cen_tile, b)
+            nc.scalar.activation(out=centres[:, t, targets], in_=h[t][:].indirect(offsets), func=COPY)
 
         first_neighbour(0)
         make_plane(1, weights[1], (4, 5), relu_vector)
+        weights.append(quantize_w1(3))
         second_neighbour(0)
         first_neighbour(1)
         make_plane(2, weights[2], (6,), relu_scalar)
         make_plane(3, weights[3], (7,), relu_scalar)
         second_neighbour(1)
+        sums = sb.tile([P, PACK, V], F32, name="w1_3_scales", align_bytes=64)
         third_neighbour(0)
         third_neighbour(1)
         for step in (first_neighbour, second_neighbour):
@@ -176,31 +181,36 @@ def tile_picked_sagecat_mean_p_kernel(
         third_neighbour(2)
         for b in range(HALVES):
             third_neighbour(3, b)
-        centres = sb.tile([P, PACK, V], BF16, name="two1", align_bytes=64)
-        for t in range(PACK):
+        centres = sb.tile([P, PACK, V], BF16, name="two0", align_bytes=64)
+        for t in range(PACK - 1):
             centre(t)
+        for b in range(HALVES):
+            centre(PACK - 1, b)
 
-        z_values = sb.tile([P, V, PACK], BF16, name="z_values", align_bytes=64)
+        z_values = [sb.tile([P, P, PACK], BF16, name="z_values%d" % b, align_bytes=64) for b in range(HALVES)]
         g_values = [sb.tile([P, P, PACK], BF16, name="g_values%d" % b, align_bytes=64) for b in range(HALVES)]
+        z_planes = [sums[:, :, half(b)].rearrange("p t v -> p v t") for b in range(HALVES)]
+        nc.vector.tensor_scalar_mul(z_values[0][:], z_planes[0], 1.0 / NEIGHBOURS)
+        nc.scalar.activation(out=z_values[1][:], in_=z_planes[1], func=COPY, scale=1.0 / NEIGHBOURS)
         for b in range(HALVES):
-            nc.vector.tensor_scalar_mul(
-                z_values[:, half(b)], sums[:, :, half(b)].rearrange("p t v -> p v t"), 1.0 / NEIGHBOURS
-            )
-        z_codes = sb.tile([P, V], U32, name="z_codes", align_bytes=64)
-        z_scales = sb.tile([P, V], U8, name="z_scales", align_bytes=64)
-        nc.scalar.copy(g_values[1][:], centres[:, :, half(1)].rearrange("p t v -> p v t"))
-        nc.vector.tensor_copy(g_values[0][:], centres[:, :, half(0)].rearrange("p t v -> p v t"))
-        nc.vector.quantize_mx(
-            out=z_codes[:].bitcast(FP8X4), scales=z_scales[:], in_=z_values[:].rearrange("p v t -> p (v t)")
-        )
+            nc.vector.tensor_copy(g_values[b][:], centres[:, :, half(b)].rearrange("p t v -> p v t"))
         groups = [bank(number, [P, P]) for number in (0, 1)]
-        for b in range(HALVES):
-            mx_pass(groups[b][:], w3, (z_codes[:, half(b)], z_scales[:, half(b)]), True, False)
-        for b in (1, 0):
+
+        def z_pass(b, start):
+            codes = sb.tile([P, P], U32, name="z_codes1" if b else "h3", align_bytes=64)
+            z = quantize(z_values[b][:].rearrange("p v t -> p (v t)"), codes[:], "z%d" % b)
+            mx_pass(groups[b][:], w3, z, start, not start)
+
+        def g_pass(b, start):
             codes = sb.tile([P, P], U32, name="g_codes%d" % b, align_bytes=64)
             g = quantize(g_values[b][:].rearrange("p v t -> p (v t)"), codes[:], "g%d" % b)
-            mx_pass(groups[b][:], w2, g, False, True)
-        for b, copy, queue in ((1, nc.scalar.copy, nc.scalar), (0, nc.vector.tensor_copy, nc.sync)):
+            mx_pass(groups[b][:], w2, g, start, not start)
+
+        z_pass(0, True)
+        g_pass(0, False)
+        g_pass(1, True)
+        z_pass(1, False)
+        for b, copy, queue in ((0, nc.scalar.copy, nc.scalar), (1, nc.vector.tensor_copy, nc.sync)):
             result = sb.tile([P, P], F32, name="result%d" % b)
             copy(result[:], groups[b][:])
             queue.dma_start(out=out[:, half(b)], in_=result[:])

@@ -115,7 +115,7 @@ def tile_picked_sagecat_mean_p_kernel(
             )
 
         def quantize_w1(t):
-            codes = sb.tile([P, P], U32, name="w1_codes%d" % (1 if t == 3 else t), align_bytes=64)
+            codes = sb.tile([P, P], U32, name="w1_codes%d" % t, align_bytes=64)
             return quantize(rounded[t // 2][:, t % 2].rearrange("p m j -> p (m j)"), codes[:], "w1_%d" % t)
 
         h = {}
@@ -126,29 +126,31 @@ def tile_picked_sagecat_mean_p_kernel(
         def relu_vector(dst, acc):
             nc.vector.tensor_scalar_max(dst, acc, 0.0)
 
-        def make_plane(t, weights, banks, relu):
-            width = S // len(banks)
-            h[t] = sb.tile([P, S], F32, name="w1_rounded1" if t == 2 else "h%d" % t, align_bytes=64)
-            for piece, number in enumerate(banks):
-                entries = slice(piece * width, (piece + 1) * width)
-                acc = bank(number, [P, width])
-                mx_pass(acc[:], weights, (picked_words[:, entries], picked_scales[:, entries]), True, True)
-                relu(h[t][:, entries], acc[:])
+        def make_part(t, first, width, number, relu):
+            entries = slice(first, first + width)
+            acc = bank(number, [P, width])
+            mx_pass(acc[:], weights[t], (picked_words[:, entries], picked_scales[:, entries]), True, True)
+            relu(h[t][:, entries], acc[:])
+
+        def new_plane(t, name):
+            h[t] = sb.tile([P, S], F32, name=name, align_bytes=64)
 
         for first in (0, 2):
             nc.scalar.activation(func=COPY, **rounding(0, first, 2))
         nc.vector.tensor_copy(**rounding(1, 0, 1))
-        weights0 = quantize_w1(0)
+        weights = {0: quantize_w1(0)}
         nc.vector.tensor_copy(**rounding(1, 1, 1))
         nc.scalar.activation(func=COPY, **rounding(1, 2, 2))
-        make_plane(0, weights0, (0, 1, 2, 3), relu_scalar)
-        weights = [weights0] + [quantize_w1(t) for t in (1, 2)]
+        new_plane(0, "h0")
+        for piece in range(4):
+            make_part(0, piece * P, P, piece, relu_scalar)
+        weights.update((t, quantize_w1(t)) for t in (1, 3, 2))
 
         one = {}
         two = [sb.tile([P, V], F32, name="two%d" % t, align_bytes=64) for t in range(PACK)]
 
         def first_neighbour(t):
-            one[t] = sb.tile([P, V], F32, name="w1_codes1" if t == 2 else "one%d" % t, align_bytes=64)
+            one[t] = sb.tile([P, V], F32, name="w1_codes3" if t == 2 else "one%d" % t, align_bytes=64)
             nc.scalar.activation(out=one[t][:], in_=h[t][:].indirect(pos_tiles[0][:]), func=COPY)
 
         def second_neighbour(t):
@@ -165,12 +167,16 @@ def tile_picked_sagecat_mean_p_kernel(
             nc.scalar.activation(out=centres[:, t, targets], in_=h[t][:].indirect(offsets), func=COPY)
 
         first_neighbour(0)
-        make_plane(1, weights[1], (4, 5), relu_vector)
-        weights.append(quantize_w1(3))
+        new_plane(1, "w1_rounded1")
+        for piece in range(2):
+            make_part(1, piece * V, V, 4 + piece, relu_vector)
+        new_plane(3, "h3")
+        make_part(3, 0, V, 6, relu_vector)
         second_neighbour(0)
         first_neighbour(1)
-        make_plane(2, weights[2], (6,), relu_scalar)
-        make_plane(3, weights[3], (7,), relu_scalar)
+        new_plane(2, "h2")
+        make_part(2, 0, S, 4, relu_scalar)
+        make_part(3, V, V, 6, relu_scalar)
         second_neighbour(1)
         sums = sb.tile([P, PACK, V], F32, name="w1_3_scales", align_bytes=64)
         third_neighbour(0)
@@ -190,7 +196,8 @@ def tile_picked_sagecat_mean_p_kernel(
         z_values = [sb.tile([P, P, PACK], BF16, name="z_values%d" % b, align_bytes=64) for b in range(HALVES)]
         g_values = [sb.tile([P, P, PACK], BF16, name="g_values%d" % b, align_bytes=64) for b in range(HALVES)]
         z_planes = [sums[:, :, half(b)].rearrange("p t v -> p v t") for b in range(HALVES)]
-        nc.vector.tensor_scalar_mul(z_values[0][:], z_planes[0], 1.0 / NEIGHBOURS)
+        nc.vector.tensor_scalar_mul(z_values[0][:, :80], z_planes[0][:, :80], 1.0 / NEIGHBOURS)
+        nc.scalar.activation(out=z_values[0][:, 80:], in_=z_planes[0][:, 80:], func=COPY, scale=1.0 / NEIGHBOURS)
         nc.scalar.activation(out=z_values[1][:], in_=z_planes[1], func=COPY, scale=1.0 / NEIGHBOURS)
         for b in range(HALVES):
             nc.vector.tensor_copy(g_values[b][:], centres[:, :, half(b)].rearrange("p t v -> p v t"))

@@ -195,12 +195,18 @@ def tile_picked_sagecat_mean_p_kernel(
 
         z_values = [sb.tile([P, P, PACK], BF16, name="z_values%d" % b, align_bytes=64) for b in range(HALVES)]
         g_values = [sb.tile([P, P, PACK], BF16, name="g_values%d" % b, align_bytes=64) for b in range(HALVES)]
-        z_planes = [sums[:, :, half(b)].rearrange("p t v -> p v t") for b in range(HALVES)]
-        nc.vector.tensor_scalar_mul(z_values[0][:, :80], z_planes[0][:, :80], 1.0 / NEIGHBOURS)
-        nc.scalar.activation(out=z_values[0][:, 80:], in_=z_planes[0][:, 80:], func=COPY, scale=1.0 / NEIGHBOURS)
-        nc.scalar.activation(out=z_values[1][:], in_=z_planes[1], func=COPY, scale=1.0 / NEIGHBOURS)
+        def weave(values, planes, b, first, last, run):
+            dst = values[b][:, first:last].rearrange("p (c i) t -> p c t i", i=run)
+            src = planes[:, :, b * P + first : b * P + last].rearrange("p t (c i) -> p c t i", i=run)
+            return dst, src
+
+        dst, src = weave(z_values, sums, 0, 0, 80, 2)
+        nc.vector.tensor_scalar_mul(dst, src, 1.0 / NEIGHBOURS)
+        for b, first in ((0, 80), (1, 0)):
+            dst, src = weave(z_values, sums, b, first, P, 2)
+            nc.scalar.activation(out=dst, in_=src, func=COPY, scale=1.0 / NEIGHBOURS)
         for b in range(HALVES):
-            nc.vector.tensor_copy(g_values[b][:], centres[:, :, half(b)].rearrange("p t v -> p v t"))
+            nc.vector.tensor_copy(*weave(g_values, centres, b, 0, P, 4))
         groups = [bank(number, [P, P]) for number in (0, 1)]
 
         def z_pass(b, start):

@@ -29,8 +29,8 @@ def load_words(queue, tile, words):
 
 def load_scales(nc, rows_out, scales):
     rows = scales[0].bitcast(I32)
-    for q in range(4):
-        nc.sync.dma_start(out=rows_out[32 * q : 32 * q + 4].bitcast(I32), in_=rows[4 * q : 4 * q + 4])
+    for r in range(4):
+        nc.sync.dma_start(out=rows_out.bitcast(I32)[r:P:32], in_=rows[r:16:4])
 
 
 def load_list(nc, pool, entries, name):
@@ -66,7 +66,7 @@ def tile_picked_sagecat_mean_p_kernel(
         x_word_tile = sb.tile([P, T], I32, name="x_word_tile", align_bytes=64)
         load_words(nc.scalar, x_word_tile, x_words)
         offs_tile = load_list(nc, sb, offs, "offs_tile")
-        load_scales(nc, x_scale_tile, x_scales)
+        load_scales(nc, x_scale_tile[:], x_scales)
         w1_rows = w1.rearrange("(p a j) c -> a p j c", a=2, j=2)
         w1_raw = []
         for a in range(2):

@@ -27,10 +27,10 @@ def load_words(queue, tile, words):
     queue.dma_start(out=tile[:], in_=words[0].rearrange("p n t -> p (n t)").bitcast(I32))
 
 
-def load_scales(nc, rows_out, scales):
+def load_scales(queues, rows_out, scales):
     rows = scales[0].bitcast(I32)
-    for r in range(4):
-        nc.sync.dma_start(out=rows_out.bitcast(I32)[r:P:32], in_=rows[r:16:4])
+    for r, queue in enumerate(queues):
+        queue.dma_start(out=rows_out.bitcast(I32)[r:P:32], in_=rows[r:16:4])
 
 
 def load_list(nc, pool, entries, name):
@@ -66,7 +66,7 @@ def tile_picked_sagecat_mean_p_kernel(
         x_word_tile = sb.tile([P, T], I32, name="x_word_tile", align_bytes=64)
         load_words(nc.scalar, x_word_tile, x_words)
         offs_tile = load_list(nc, sb, offs, "offs_tile")
-        load_scales(nc, x_scale_tile[:], x_scales)
+        load_scales((nc.sync, nc.scalar, nc.sync, nc.scalar), x_scale_tile[:], x_scales)
         w1_rows = w1.rearrange("(p a j) c -> a p j c", a=2, j=2)
         w1_raw = []
         for a in range(2):
@@ -80,7 +80,7 @@ def tile_picked_sagecat_mean_p_kernel(
             word_tile = sb.tile([P, N], I32, name="last_words%d" % i, align_bytes=64)
             load_words(nc.sync, word_tile, words)
             scale_columns = last_scales[:, i * N : (i + 1) * N]
-            load_scales(nc, scale_columns, scales)
+            load_scales((nc.sync,) * 4, scale_columns, scales)
             last_weights.append((word_tile[:], scale_columns))
         w2, w3 = last_weights
 

@@ -27,9 +27,9 @@ def load_words(queue, tile, words):
     queue.dma_start(out=tile[:], in_=words[0].rearrange("p n t -> p (n t)").bitcast(I32))
 
 
-def load_scales(queues, rows_out, scales):
+def load_scales(queues, rows_out, scales, first=0):
     rows = scales[0].bitcast(I32)
-    for r, queue in enumerate(queues):
+    for r, queue in enumerate(queues, first):
         queue.dma_start(out=rows_out.bitcast(I32)[r:P:32], in_=rows[r:16:4])
 
 
@@ -66,12 +66,14 @@ def tile_picked_sagecat_mean_p_kernel(
         x_word_tile = sb.tile([P, T], I32, name="x_word_tile", align_bytes=64)
         load_words(nc.scalar, x_word_tile, x_words)
         offs_tile = load_list(nc, sb, offs, "offs_tile")
-        load_scales((nc.sync, nc.scalar, nc.sync, nc.scalar), x_scale_tile[:], x_scales)
+        load_scales((nc.sync,) * 3, x_scale_tile[:], x_scales)
         w1_rows = w1.rearrange("(p a j) c -> a p j c", a=2, j=2)
         w1_raw = []
         for a in range(2):
+            if a == 1:
+                load_scales((nc.scalar,), x_scale_tile[:], x_scales, 3)
             raw = sb.tile([P, 2, H], F32, name="w1_raw%d" % a)
-            nc.sync.dma_start(out=raw[:], in_=w1_rows[a])
+            nc.scalar.dma_start(out=raw[:], in_=w1_rows[a])
             w1_raw.append(raw)
         pos_tiles = [load_list(nc, sb, pos, "pos_tile%d" % d) for d, pos in enumerate((pos1, pos2, pos3))]
         cen_tile = load_list(nc, sb, cen, "cen_tile")

@@ -202,9 +202,9 @@ def tile_picked_sagecat_mean_p_kernel(
             src = planes[:, :, b * P + first : b * P + last].rearrange("p t (c i) -> p c t i", i=run)
             return dst, src
 
-        dst, src = weave(z_values, sums, 0, 0, 80, 2)
+        dst, src = weave(z_values, sums, 0, 0, 48, 2)
         nc.vector.tensor_scalar_mul(dst, src, 1.0 / NEIGHBOURS)
-        for b, first in ((0, 80), (1, 0)):
+        for b, first in ((0, 48), (1, 0)):
             dst, src = weave(z_values, sums, b, first, P, 2)
             nc.scalar.activation(out=dst, in_=src, func=COPY, scale=1.0 / NEIGHBOURS)
         for b in range(HALVES):

@@ -66,14 +66,13 @@ def tile_picked_sagecat_mean_p_kernel(
         x_word_tile = sb.tile([P, T], I32, name="x_word_tile", align_bytes=64)
         load_words(nc.scalar, x_word_tile, x_words)
         offs_tile = load_list(nc, sb, offs, "offs_tile")
-        load_scales((nc.sync,) * 3, x_scale_tile[:], x_scales)
         w1_rows = w1.rearrange("(p a j) c -> a p j c", a=2, j=2)
         w1_raw = []
         for a in range(2):
             if a == 1:
-                load_scales((nc.scalar,), x_scale_tile[:], x_scales, 3)
+                load_scales((nc.sync, nc.scalar) * 2, x_scale_tile[:], x_scales)
             raw = sb.tile([P, 2, H], F32, name="w1_raw%d" % a)
-            nc.scalar.dma_start(out=raw[:], in_=w1_rows[a])
+            nc.sync.dma_start(out=raw[:], in_=w1_rows[a])
             w1_raw.append(raw)
         pos_tiles = [load_list(nc, sb, pos, "pos_tile%d" % d) for d, pos in enumerate((pos1, pos2, pos3))]
         cen_tile = load_list(nc, sb, cen, "cen_tile")

@@ -27,9 +27,9 @@ def load_words(queue, tile, words):
     queue.dma_start(out=tile[:], in_=words[0].rearrange("p n t -> p (n t)").bitcast(I32))
 
 
-def load_scales(queues, rows_out, scales, first=0):
+def load_scales(queues, rows_out, scales):
     rows = scales[0].bitcast(I32)
-    for r, queue in enumerate(queues, first):
+    for r, queue in enumerate(queues):
         queue.dma_start(out=rows_out.bitcast(I32)[r:P:32], in_=rows[r:16:4])
 
 
@@ -70,20 +70,20 @@ def tile_picked_sagecat_mean_p_kernel(
         w1_raw = []
         for a in range(2):
             if a == 1:
-                load_scales((nc.sync, nc.scalar) * 2, x_scale_tile[:], x_scales)
+                load_scales((nc.sync,) * 4, x_scale_tile[:], x_scales)
             raw = sb.tile([P, 2, H], F32, name="w1_raw%d" % a)
             nc.sync.dma_start(out=raw[:], in_=w1_rows[a])
             w1_raw.append(raw)
         pos_tiles = [load_list(nc, sb, pos, "pos_tile%d" % d) for d, pos in enumerate((pos1, pos2, pos3))]
         cen_tile = load_list(nc, sb, cen, "cen_tile")
         last_weights = []
-        for i, (words, scales) in enumerate(((w2_words, w2_scales), (w3_words, w3_scales))):
+        for i, (words, scales) in enumerate(((w3_words, w3_scales), (w2_words, w2_scales))):
             word_tile = sb.tile([P, N], I32, name="last_words%d" % i, align_bytes=64)
             load_words(nc.sync, word_tile, words)
             scale_columns = last_scales[:, i * N : (i + 1) * N]
             load_scales((nc.sync,) * 4, scale_columns, scales)
             last_weights.append((word_tile[:], scale_columns))
-        w2, w3 = last_weights
+        w3, w2 = last_weights
 
         def quantize(values, codes, name):
             scales = sb.tile([P, P], U8, name=name + "_scales", align_bytes=64)

@@ -220,8 +220,8 @@ def tile_picked_sagecat_mean_p_kernel(
             g = quantize(g_values[b][:].rearrange("p v t -> p (v t)"), codes[:], "g%d" % b)
             mx_pass(groups[b][:], w2, g, start, not start)
 
-        z_pass(0, True)
-        g_pass(0, False)
+        g_pass(0, True)
+        z_pass(0, False)
         g_pass(1, True)
         z_pass(1, False)
         for b, copy, queue in ((0, nc.scalar.copy, nc.scalar), (1, nc.vector.tensor_copy, nc.sync)):

@@ -165,7 +165,7 @@ def tile_picked_sagecat_mean_p_kernel(
         def centre(t, b=None):
             targets = slice(0, V) if b is None else half(b)
             offsets = cen_tile[:] if b is None else list_half(cen_tile, b)
-            nc.scalar.activation(out=centres[:, t, targets], in_=h[t][:].indirect(offsets), func=COPY)
+            nc.scalar.activation(out=centres[:, t // 2, targets, t % 2], in_=h[t][:].indirect(offsets), func=COPY)
 
         first_neighbour(0)
         new_plane(1, "w1_rounded1")
@@ -188,7 +188,7 @@ def tile_picked_sagecat_mean_p_kernel(
         third_neighbour(2)
         for b in range(HALVES):
             third_neighbour(3, b)
-        centres = sb.tile([P, PACK, V], BF16, name="two0", align_bytes=64)
+        centres = sb.tile([P, 2, V, 2], BF16, name="two0", align_bytes=64)
         for t in range(PACK - 1):
             centre(t)
         for b in range(HALVES):
@@ -201,13 +201,15 @@ def tile_picked_sagecat_mean_p_kernel(
             src = planes[:, :, b * P + first : b * P + last].rearrange("p t (c i) -> p c t i", i=run)
             return dst, src
 
-        dst, src = weave(z_values, sums, 0, 0, 48, 2)
+        dst, src = weave(z_values, sums, 0, 0, 80, 2)
         nc.vector.tensor_scalar_mul(dst, src, 1.0 / NEIGHBOURS)
-        for b, first in ((0, 48), (1, 0)):
+        for b, first in ((0, 80), (1, 0)):
             dst, src = weave(z_values, sums, b, first, P, 2)
             nc.scalar.activation(out=dst, in_=src, func=COPY, scale=1.0 / NEIGHBOURS)
         for b in range(HALVES):
-            nc.vector.tensor_copy(*weave(g_values, centres, b, 0, P, 4))
+            dst = g_values[b][:].bitcast(I32).rearrange("p (c i) u -> p c u i", i=2)
+            src = centres[:].bitcast(I32)[:, :, half(b), 0].rearrange("p u (c i) -> p c u i", i=2)
+            nc.vector.tensor_copy(dst, src)
         groups = [bank(number, [P, P]) for number in (0, 1)]
 
         def z_pass(b, start):

@@ -15,6 +15,7 @@ FP8X4 = mybir.dt.float8_e4m3fn_x4
 COPY = mybir.ActivationFunctionType.Copy
 RELU = mybir.ActivationFunctionType.Relu
 ADD = mybir.AluOpType.add
+MULT = mybir.AluOpType.mult
 
 P = 128
 PACK = 4
@@ -108,11 +109,12 @@ def tile_picked_sagecat_mean_p_kernel(
 
         rounded = [sb.tile([P, 2, P, PACK], BF16, name="w1_rounded%d" % u, align_bytes=64) for u in range(2)]
 
-        def rounding(a, first, count):
+        def rounding(a, first, count, columns=slice(0, P)):
             dst = rounded[first // 2][:].rearrange("p e m j -> p m e j")
             src = w1_raw[a][:].rearrange("p j (m t) -> p m t j", t=PACK)
             return dict(
-                out=dst[:, :, first % 2 : first % 2 + count, 2 * a : 2 * a + 2], in_=src[:, :, first : first + count]
+                out=dst[:, columns, first % 2 : first % 2 + count, 2 * a : 2 * a + 2],
+                in_=src[:, columns, first : first + count],
             )
 
         def quantize_w1(t):
@@ -136,9 +138,11 @@ def tile_picked_sagecat_mean_p_kernel(
         def new_plane(t, name):
             h[t] = sb.tile([P, S], F32, name=name, align_bytes=64)
 
-        for first in (0, 2):
-            nc.scalar.activation(func=COPY, **rounding(0, first, 2))
-        nc.vector.tensor_copy(**rounding(1, 0, 1))
+        nc.scalar.activation(func=COPY, **rounding(0, 0, 2))
+        late = rounding(0, 2, 2)
+        nc.gpsimd.tensor_scalar(late["out"], late["in_"], 1.0, 0.0, MULT, ADD)
+        nc.scalar.activation(func=COPY, **rounding(1, 0, 1, slice(0, P // 2)))
+        nc.vector.tensor_copy(**rounding(1, 0, 1, slice(P // 2, P)))
         weights = {0: quantize_w1(0)}
         nc.vector.tensor_copy(**rounding(1, 1, 1))
         nc.scalar.activation(func=COPY, **rounding(1, 2, 2))

from contextlib import ExitStack

import concourse.mybir as mybir

K, T, S, V, H, N = 512, 1024, 512, 256, 512, 128
FLOPS = 2 * K * H * S + 2 * 2 * H * N * V

F32 = mybir.dt.float32
BF16 = mybir.dt.bfloat16
I32 = mybir.dt.int32
U32 = mybir.dt.uint32
U16 = mybir.dt.uint16
U8 = mybir.dt.uint8
FP8X4 = mybir.dt.float8_e4m3fn_x4
COPY = mybir.ActivationFunctionType.Copy
RELU = mybir.ActivationFunctionType.Relu
ADD = mybir.AluOpType.add
MULT = mybir.AluOpType.mult

P = 128
PACK = 4
HALVES = V // P
NEIGHBOURS = 3
PER_COLUMN = 16


def load_words(queue, tile, words):
    queue.dma_start(out=tile[:], in_=words[0].rearrange("p n t -> p (n t)").bitcast(I32))


def load_scales(queues, rows_out, scales):
    rows = scales[0].bitcast(I32)
    for r, queue in enumerate(queues):
        queue.dma_start(out=rows_out.bitcast(I32)[r:P:32], in_=rows[r:16:4])


def load_list(nc, pool, entries, name):
    tile = pool.tile(list(entries.shape), U16, name=name)
    nc.sync.dma_start(tile[:], entries)
    return tile


def half(b):
    return slice(b * P, (b + 1) * P)


def list_half(tile, b):
    return tile[:, b * P // PER_COLUMN : (b + 1) * P // PER_COLUMN]


def tile_picked_sagecat_mean_p_kernel(
    tc, x_words, x_scales, w1, w2_words, w2_scales, w3_words, w3_scales, offs, cen, pos1, pos2, pos3, out
):
    nc = tc.nc
    with ExitStack() as ctx:
        sb = ctx.enter_context(tc.tile_pool(name="sb", bufs=1))
        ps = ctx.enter_context(tc.psum_pool(name="ps", bufs=1))

        def bank(number, shape):
            return ps.tile(shape, F32, name="bank%d" % number)

        x_scale_tile = sb.tile([P, T], U8, name="x_scale_tile", align_bytes=64)
        nc.vector.memset(x_scale_tile[:].bitcast(I32), 0)
        last_scales = sb.tile([P, 2 * N], U8, name="last_scales", align_bytes=64)
        nc.vector.memset(last_scales[:].bitcast(I32), 0)

        x_word_tile = sb.tile([P, T], I32, name="x_word_tile", align_bytes=64)
        load_words(nc.scalar, x_word_tile, x_words)
        offs_tile = load_list(nc, sb, offs, "offs_tile")
        w1_rows = w1.rearrange("(p a j) c -> a p j c", a=2, j=2)
        w1_raw = []
        for a in range(2):
            if a == 1:
                load_scales((nc.sync,) * 4, x_scale_tile[:], x_scales)
            raw = sb.tile([P, 2, H], F32, name="w1_raw%d" % a)
            nc.sync.dma_start(out=raw[:], in_=w1_rows[a])
            w1_raw.append(raw)
        pos_tiles = [load_list(nc, sb, pos, "pos_tile%d" % d) for d, pos in enumerate((pos1, pos2, pos3))]
        cen_tile = load_list(nc, sb, cen, "cen_tile")
        last_weights = []
        for i, (words, scales) in enumerate(((w3_words, w3_scales), (w2_words, w2_scales))):
            word_tile = sb.tile([P, N], I32, name="last_words%d" % i, align_bytes=64)
            load_words(nc.sync, word_tile, words)
            scale_columns = last_scales[:, i * N : (i + 1) * N]
            load_scales((nc.sync,) * 4, scale_columns, scales)
            last_weights.append((word_tile[:], scale_columns))
        w3, w2 = last_weights

        def quantize(values, codes, name):
            scales = sb.tile([P, P], U8, name=name + "_scales", align_bytes=64)
            nc.vector.quantize_mx(out=codes.bitcast(FP8X4), scales=scales[:], in_=values)
            return codes, scales[:]

        def mx_pass(acc, stationary, moving, start, stop):
            nc.tensor.matmul_mx(
                out=acc,
                lhsT=stationary[0].bitcast(FP8X4),
                lhsT_scale=stationary[1],
                rhs=moving[0].bitcast(FP8X4),
                rhs_scale=moving[1],
                start=start,
                stop=stop,
            )

        picked_words = sb.tile([P, S], U32, name="picked_words", align_bytes=64)
        picked_scales = sb.tile([P, S], U8, name="picked_scales", align_bytes=64)
        nc.vector.tensor_copy(picked_words[:], x_word_tile[:].bitcast(U32).indirect(offs_tile[:]))
        nc.vector.tensor_copy(picked_scales[:], x_scale_tile[:].indirect(offs_tile[:]))

        rounded = [sb.tile([P, 2, P, PACK], BF16, name="w1_rounded%d" % u, align_bytes=64) for u in range(2)]

        def rounding(a, first, count, columns=slice(0, P)):
            dst = rounded[first // 2][:].rearrange("p e m j -> p m e j")
            src = w1_raw[a][:].rearrange("p j (m t) -> p m t j", t=PACK)
            return dict(
                out=dst[:, columns, first % 2 : first % 2 + count, 2 * a : 2 * a + 2],
                in_=src[:, columns, first : first + count],
            )

        def quantize_w1(t):
            codes = sb.tile([P, P], U32, name="w1_codes%d" % t, align_bytes=64)
            return quantize(rounded[t // 2][:, t % 2].rearrange("p m j -> p (m j)"), codes[:], "w1_%d" % t)

        h = {}

        def relu_scalar(dst, acc):
            nc.scalar.activation(out=dst, in_=acc, func=RELU)

        def relu_vector(dst, acc):
            nc.vector.tensor_scalar_max(dst, acc, 0.0)

        def make_part(t, first, width, number, relu):
            entries = slice(first, first + width)
            acc = bank(number, [P, width])
            mx_pass(acc[:], weights[t], (picked_words[:, entries], picked_scales[:, entries]), True, True)
            relu(h[t][:, entries], acc[:])

        def new_plane(t, name):
            h[t] = sb.tile([P, S], F32, name=name, align_bytes=64)

        nc.scalar.activation(func=COPY, **rounding(0, 0, 2))
        late = rounding(0, 2, 2)
        nc.gpsimd.tensor_scalar(late["out"], late["in_"], 1.0, 0.0, MULT, ADD)
        nc.scalar.activation(func=COPY, **rounding(1, 0, 1, slice(0, P // 2)))
        nc.vector.tensor_copy(**rounding(1, 0, 1, slice(P // 2, P)))
        weights = {0: quantize_w1(0)}
        nc.vector.tensor_copy(**rounding(1, 1, 1))
        nc.scalar.activation(func=COPY, **rounding(1, 2, 2))
        new_plane(0, "h0")
        for piece in range(4):
            make_part(0, piece * P, P, piece, relu_scalar)
        weights.update((t, quantize_w1(t)) for t in (1, 3, 2))

        one = {}
        two = [sb.tile([P, V], F32, name="two%d" % t, align_bytes=64) for t in range(PACK)]

        def first_neighbour(t):
            one[t] = sb.tile([P, V], F32, name="w1_codes3" if t == 2 else "one%d" % t, align_bytes=64)
            nc.scalar.activation(out=one[t][:], in_=h[t][:].indirect(pos_tiles[0][:]), func=COPY)

        def second_neighbour(t):
            nc.vector.tensor_tensor(two[t][:], h[t][:].indirect(pos_tiles[1][:]), one[t][:], ADD)

        def third_neighbour(t, b=None):
            targets = slice(0, V) if b is None else half(b)
            offsets = pos_tiles[2][:] if b is None else list_half(pos_tiles[2], b)
            nc.vector.tensor_tensor(sums[:, t, targets], h[t][:].indirect(offsets), two[t][:, targets], ADD)

        def centre(t, b=None):
            targets = slice(0, V) if b is None else half(b)
            offsets = cen_tile[:] if b is None else list_half(cen_tile, b)
            nc.scalar.activation(out=centres[:, t // 2, targets, t % 2], in_=h[t][:].indirect(offsets), func=COPY)

        first_neighbour(0)
        new_plane(1, "w1_rounded1")
        for piece in range(2):
            make_part(1, piece * V, V, 4 + piece, relu_vector)
        new_plane(3, "h3")
        make_part(3, 0, V, 6, relu_vector)
        second_neighbour(0)
        first_neighbour(1)
        new_plane(2, "h2")
        make_part(2, 0, S, 4, relu_scalar)
        make_part(3, V, V, 6, relu_scalar)
        second_neighbour(1)
        sums = sb.tile([P, PACK, V], F32, name="w1_3_scales", align_bytes=64)
        third_neighbour(0)
        third_neighbour(1)
        for step in (first_neighbour, second_neighbour):
            for t in (2, 3):
                step(t)
        third_neighbour(2)
        for b in range(HALVES):
            third_neighbour(3, b)
        centres = sb.tile([P, 2, V, 2], BF16, name="two0", align_bytes=64)
        for t in range(PACK - 1):
            centre(t)
        for b in range(HALVES):
            centre(PACK - 1, b)

        z_values = [sb.tile([P, P, PACK], BF16, name="z_values%d" % b, align_bytes=64) for b in range(HALVES)]
        g_values = [sb.tile([P, P, PACK], BF16, name="g_values%d" % b, align_bytes=64) for b in range(HALVES)]
        def weave(values, planes, b, first, last, run):
            dst = values[b][:, first:last].rearrange("p (c i) t -> p c t i", i=run)
            src = planes[:, :, b * P + first : b * P + last].rearrange("p t (c i) -> p c t i", i=run)
            return dst, src

        dst, src = weave(z_values, sums, 0, 0, 80, 2)
        nc.vector.tensor_scalar_mul(dst, src, 1.0 / NEIGHBOURS)
        for b, first in ((0, 80), (1, 0)):
            dst, src = weave(z_values, sums, b, first, P, 2)
            nc.scalar.activation(out=dst, in_=src, func=COPY, scale=1.0 / NEIGHBOURS)
        for b in range(HALVES):
            dst = g_values[b][:].bitcast(I32).rearrange("p (c i) u -> p c u i", i=2)
            src = centres[:].bitcast(I32)[:, :, half(b), 0].rearrange("p u (c i) -> p c u i", i=2)
            nc.vector.tensor_copy(dst, src)
        groups = [bank(number, [P, P]) for number in (0, 1)]

        def z_pass(b, start):
            codes = sb.tile([P, P], U32, name="z_codes1" if b else "h3", align_bytes=64)
            z = quantize(z_values[b][:].rearrange("p v t -> p (v t)"), codes[:], "z%d" % b)
            mx_pass(groups[b][:], w3, z, start, not start)

        def g_pass(b, start):
            codes = sb.tile([P, P], U32, name="g_codes%d" % b, align_bytes=64)
            g = quantize(g_values[b][:].rearrange("p v t -> p (v t)"), codes[:], "g%d" % b)
            mx_pass(groups[b][:], w2, g, start, not start)

        g_pass(0, True)
        z_pass(0, False)
        g_pass(1, True)
        z_pass(1, False)
        for b, copy, queue in ((0, nc.scalar.copy, nc.scalar), (1, nc.vector.tensor_copy, nc.sync)):
            result = sb.tile([P, P], F32, name="result%d" % b)
            copy(result[:], groups[b][:])
            queue.dma_start(out=out[:, half(b)], in_=result[:])
